import numpy as np, ml_dtypes
CORES = [6,15,38,47]
N = 4
BF = ml_dtypes.bfloat16
def gentries(a):
    return np.ascontiguousarray(a.reshape(8, 16, -1).transpose(0, 2, 1)).reshape(8, -1)
def gtable(e):
    e = np.asarray(e); return np.ascontiguousarray(e.reshape(8, -1, 16).transpose(0, 2, 1)).reshape(128, -1).astype(np.int32)
W, LN, RO, BL, LG = 4096, 64, 4, 16, 12
SZ = W // LN
DIST = 1 + (np.arange(LN) // BL) % (N - 1)
ROT = (np.arange(16)[:, None] + np.arange(16)[None, :]) % 16
PAT = 255 * np.array([0, 0, 0, 0, 1, 0, 0, 1, 1, 0, 1, 0, 1, 1, 1, 1])
def parts(rng):
    x = rng.integers(0, 256, (N, 8, 16, W)); L = rng.integers(0, W, (N, 8, LN, 16)); c = rng.integers(0, W, (N, 8, LN))
    s = rng.choice(np.array([1.0, 1.3, 1.6]), (N, 8, LN, 1))
    z = np.minimum(np.maximum(np.rint(127.5 + s * (255 * rng.random((N, 8, LN, 16)) - 127.5)), 0), 255).astype(np.int64)
    return x, L, c, z
def mid(rng, x, z, q):
    a = rng.integers(0, W, 512); b = rng.integers(0, LN, 512)
    zz = np.roll(z[:, :, b, :], 5, axis=3).transpose(0, 1, 3, 2)
    d = np.sort(np.sum(np.abs(x[:, :, :, a] - zz), axis=2), axis=2)
    return np.minimum(np.maximum(np.take_along_axis(d, (q * 512).astype(np.int64)[:, :, None], 2)[:, :, 0], 1275), 2295)
def pack(x, L, c, z, t):
    return {"x": x.reshape(N, 128, W).astype(np.float32).astype(BF), "ls": np.stack([gtable(a) for a in L]), "an": c.astype(np.int32),
            "z": np.ascontiguousarray(z.transpose(0, 1, 3, 2)).reshape(N, 128, LN).astype(np.float32).astype(BF), "th": t.reshape(N, 8, 1).astype(np.int32)}
def setup_inputs(rng):
    x, L, c, z = parts(rng)
    return pack(x, L, c, z, mid(rng, x, z, rng.choice(np.array([0.15, 0.22, 0.3, 0.4]), (N, 8))))
def rough(rng, shape, share):
    e = np.minimum(np.exp2(8.1 * rng.random(shape)).astype(np.int64) - 1, 255)
    return np.where(rng.random(shape) < share, 255 - e, e)
def setup_inputs_spread(rng):
    sh = np.array([0.2, 0.5, 0.8])
    x = rough(rng, (N, 8, 16, W), rng.choice(sh, (N, 8, 1, W))); z = rough(rng, (N, 8, LN, 16), rng.choice(sh, (N, 8, LN, 1)))
    e = np.exp2(LG * rng.random((N, 8, LN, 17))).astype(np.int64) - 1
    e = np.where(rng.random(e.shape) < 0.5, W - 1 - e, e)
    return pack(x, e[..., :16], e[..., 16], z, mid(rng, x, z, 0.05 + 0.9 * rng.random((N, 8))))
def setup_inputs_ends(rng):
    sh = np.array([0.3, 0.5, 0.7])
    x = 255 * (rng.random((N, 8, 16, W)) < rng.choice(sh, (N, 8, 1, W))).astype(np.int64)
    z = 255 * (rng.random((N, 8, LN, 16)) < rng.choice(sh, (N, 8, LN, 1))).astype(np.int64)
    L = (W - 1) * (rng.random((N, 8, LN, 16)) < rng.choice(np.array([0.25, 0.5, 0.75]), (N, 8, LN, 1))).astype(np.int64)
    c = (W - 1) * rng.integers(0, 2, (N, 8, LN))
    t = np.where(rng.random((N, 8)) < 0.5, 1275, 2295); t[:, 2] = 1275; t[:, 5] = 2295
    x[:, 1::2, :, 0] = 255; x[:, 1::2, :, W - 1] = 0
    for l, a, b in ((0, 0, 0), (1, W - 1, 0), (2, 0, 255), (3, W - 1, 255), (LN - 4, 0, 0), (LN - 3, W - 1, 255), (LN - 2, W - 1, 0), (LN - 1, 0, 255)):
        L[:, 1::2, l] = 0; c[:, 1::2, l] = a; z[:, 1::2, l] = b
    return pack(x, L, c, z, t)
def setup_inputs_corners(rng):
    x, L, c, z = parts(rng); t = rng.choice(np.array([1275, 1400, 1600, 1800]), (N, 8))
    cnt = np.minimum(np.array([0, 1, 31, 32, 33, LN - 1, LN, 9]), LN)
    for q in range(N):
        order = np.arange(8) if q == 0 else rng.permutation(8)
        for g in range(8):
            hot = rng.permutation(LN) < cnt[order[g]]
            for l in range(LN):
                m = int(rng.choice(np.array([16, 16, 15, 9, 17]))) if hot[l] else int(rng.choice(np.array([8, 8, 1, 0])))
                col = SZ * l + 8 + int(rng.integers(0, 16)); kk = int(rng.choice(np.array([0, 15, int(rng.integers(0, 16))]))) if m == 16 else 0
                zz = np.full(16, 255) if m == 17 else np.roll(PAT, int(rng.integers(0, 16)))
                x[q, g][:, [col - 6, col + 1, col + 6]] = rng.integers(120, 136, (16, 3))
                x[q, g, :, col] = rng.integers(120, 136, 16) if m == 0 else np.roll(zz, -kk)
                c[q, g, l] = col; z[q, g, l] = zz
                L[q, g, l] = 0 if m in (0, 16, 17) else np.where(rng.permutation(16) < m, 0, 6)
    return pack(x, L, c, z, t)
def setup_inputs_ties(rng):
    x, L, c, z = parts(rng); t = mid(rng, x, z, rng.choice(np.array([0.2, 0.3, 0.4]), (N, 8)))
    t[:, ::2] = rng.integers(1275, 2296, (N, 4)); t[0, 0] = 1275; t[N - 1, 6] = 2295
    s = t[:, ::2, None] + rng.integers(-1, 2, (N, 4, LN)); up = rng.random((N, 4, LN)) < 0.5; m = rng.random((N, 4, LN)) < 0.6
    v = (s // 16)[:, :, None, :] + (np.arange(16)[:, None] < (s % 16)[:, :, None, :])
    v = np.where(up[:, :, None, :], 255 - v, v); col = SZ * np.arange(LN) + rng.integers(0, SZ, (N, 4, LN))
    xe = x[:, ::2]; np.put_along_axis(xe, np.repeat(col[:, :, None, :], 16, axis=2), v, 3)
    L[:, ::2] = np.where(m[..., None], 0, L[:, ::2]); c[:, ::2] = np.where(m, col, c[:, ::2]); z[:, ::2] = np.where(m[..., None], 255 * up[..., None], z[:, ::2])
    L[:, 1] = L[:, 1, :1].copy(); c[:, 1] = c[:, 1, :1].copy(); z[:, 1] = z[:, 1][:, np.arange(LN) % 2]
    L[:, 3] = 0; c[:, 3] = W - 1; c[1::2, 3, LN - 1] = 0
    L[:, 5] = rng.choice(np.array([0, 3, W // 2, W - 1]), (N, LN, 16))
    x[:, 7, :, 1::2] = x[:, 7, :, ::2].copy(); L[:, 7, 1::2] = L[:, 7, ::2].copy(); c[:, 7, 1::2] = c[:, 7, ::2].copy()
    return pack(x, L, c, z, t)
def check_inputs(d):
    bad = []
    for k, lo, hi in (("x", 0, 255), ("ls", 0, W - 1), ("an", 0, W - 1), ("z", 0, 255), ("th", 1275, 2295)):
        v = np.asarray(d[k]).astype(np.float64)
        if not (np.min(v) >= lo and np.max(v) <= hi): bad.append("range of " + k)
        elif np.any(v != np.floor(v)): bad.append("whole numbers in " + k)
    return bad
def reference(x, ls, an, z, th):
    X = x.astype(np.float32).astype(np.int64).reshape(N, 8, 16, W)
    L = np.stack([gentries(a) for a in ls]).astype(np.int64).reshape(N, 8, LN, 16)
    c = an.astype(np.int64)
    Z = z.astype(np.float32).astype(np.int64).reshape(N, 8, 16, LN).transpose(0, 1, 3, 2)
    t = th.astype(np.int64).reshape(N, 8); A = np.zeros((N, 8), np.int64)
    src = ((np.arange(N)[:, None] - DIST[None, :]) % N)[:, None, :]; gg = np.arange(8)[None, :, None]; sl = np.arange(LN)[None, None, :]
    k16 = np.arange(16)
    for rnd in range(RO):
        La = L[:, :, :, ROT]; Li = L[:, :, :, None, :]
        E = (((La * Li) >> 5) + La - Li + c[:, :, :, None, None]) & (W - 1)
        ix = E.reshape(N, 8, LN * 256); D = np.zeros(E.shape, np.int64)
        for f in range(16):
            D = D + np.abs(np.take_along_axis(X[:, :, f], ix, 2).reshape(E.shape) - Z[:, :, :, (f + k16) % 16][..., None])
        C = np.sum(D < (t + (A & 31))[:, :, None, None, None], axis=4)
        kt = np.argmax(C, axis=3); kb = np.argmin(C, axis=3)
        win = np.take_along_axis(E, kt[..., None, None], 3)[:, :, :, 0]
        v = np.take_along_axis(np.take_along_axis(E, kb[..., None, None], 3)[:, :, :, 0], kt[..., None], 3)
        M = np.max(np.take_along_axis(X, np.repeat(win.reshape(N, 8, 1, LN * 16), 16, axis=2), 3).reshape(N, 8, 16, LN, 16), axis=4).transpose(0, 1, 3, 2)
        Y = (M + Z) >> 1
        u = np.sum(Y * (2 * k16 + 1), axis=3) & (W - 1)
        A = np.sum(np.max(C, axis=3) >= 9, axis=2)
        place = SZ * np.arange(LN) + (u & (SZ - 1))
        np.put_along_axis(X, np.repeat(place[:, :, None, :], 16, axis=2), Y.transpose(0, 1, 3, 2), 3)
        c = (((u * u) >> 5) + 37 * u + A[:, :, None]) & (W - 1)
        Z = np.abs(Z - M)
        L = np.where(np.roll(k16 == kb[..., None], 1, axis=0), np.roll(v, 1, axis=0), win)
        L = L[src, gg, sl]; c = c[src, gg, sl]; Z = Z[src, gg, sl]
    return {"yx": X.reshape(N, 128, W).astype(np.float32).astype(BF), "yl": np.stack([gtable(a) for a in L]).astype(np.float32), "ya": c.astype(np.float32),
            "yz": np.ascontiguousarray(Z.transpose(0, 1, 3, 2)).reshape(N, 128, LN).astype(np.float32).astype(BF)}

@@ -1,0 +1,520 @@
+from concourse.bass import DstId, RemoteDMATransfer
+from concourse.mybir import AluOpType as Op, ActivationFunctionType as Act
+
+RO = 4
+ORD = [2, 0, 3, 1]
+NT = 8
+S_T, V_T = 0.224, 0.262
+V_LATE = [0.0, 1.9, 1.9, 1.9]
+S_BEST = 48
+
+SCRATCH = {
+    "tab": ("sbuf", [128, NT * 4096], "bfloat16"),
+    "sd": ("sbuf", [128, 112 * 128], "bfloat16"),
+    "vd": ("sbuf", [128, 96 * 128], "bfloat16"),
+    "vr": ("sbuf", [128, 96 * 128], "bfloat16"),
+    "W": ("sbuf", [128, 1024], "int32"), "E": ("sbuf", [128, 1024], "int32"),
+    "off0": ("sbuf", [128, 512], "uint16"), "off1": ("sbuf", [128, 512], "uint16"),
+    "L16": ("sbuf", [128, 64], "float16"), "B": ("sbuf", [128, 64], "float32"),
+    "C0": ("sbuf", [128, 64], "float32"),
+    "zb": ("sbuf", [128, 64], "bfloat16"), "z8": ("sbuf", [128, 64], "bfloat16"), "zh": ("sbuf", [128, 64], "float32"),
+    "thr": ("sbuf", [128, 512], "float16"), "nT": ("sbuf", [128, 1], "float32"), "ncol": ("sbuf", [128, 1], "float32"),
+    "kA": ("sbuf", [128, 1], "float32"), "Ai": ("sbuf", [128, 1], "int32"), "Aj": ("sbuf", [128, 1], "int32"),
+    "cmp0": ("sbuf", [128, 512], "bfloat16"), "cmp1": ("sbuf", [128, 512], "bfloat16"),
+    "En": ("sbuf", [128, 128], "float32"), "Sc": ("sbuf", [128, 128], "float32"),
+    "hot": ("sbuf", [128, 4], "bfloat16"),
+    "KI": ("sbuf", [128, 8], "int32"), "KJ": ("sbuf", [128, 8], "int32"), "koff": ("sbuf", [128, 8], "uint16"),
+    "EtU": ("sbuf", [128, 128], "uint16"), "OO": ("sbuf", [128, 128], "bfloat16"),
+    "Eb": ("sbuf", [128, 64], "float32"), "Q": ("sbuf", [128, 64], "float16"),
+    "G": ("sbuf", [128, 1024], "bfloat16"), "Ms": ("sbuf", [128, 1024], "bfloat16"),
+    "Yi": ("sbuf", [128, 64], "int32"), "Yb": ("sbuf", [128, 64], "bfloat16"), "Yr": ("sbuf", [128, 512], "bfloat16"),
+    "dz": ("sbuf", [128, 64], "float32"),
+    "si": ("sbuf", [128, 64], "int32"), "ui": ("sbuf", [128, 64], "int32"), "u1": ("sbuf", [128, 64], "float32"),
+    "u2": ("sbuf", [128, 64], "float32"), "Wc": ("sbuf", [128, 64], "int32"), "Wd": ("sbuf", [128, 64], "int32"),
+    "w6": ("sbuf", [128, 64], "int32"), "wv": ("sbuf", [128, 64], "float32"), "ws": ("sbuf", [128, 64], "float32"),
+    "woff": ("sbuf", [128, 4], "uint16"),
+    "tm": ("sbuf", [128, 64], "float16"),
+    "Lc": ("sbuf", [128, 32], "float16"),
+    "J": ("sbuf", [128, 16], "int32"), "J2": ("sbuf", [128, 16], "int32"), "tg": ("sbuf", [128, 16], "float32"),
+    "mi": ("sbuf", [128, 128], "int32"), "mh": ("sbuf", [128, 128], "float16"), "ms": ("sbuf", [128, 128], "int32"),
+    "pi": ("sbuf", [128, 1], "int32"), "pj": ("sbuf", [128, 1], "int32"), "pk": ("sbuf", [128, 1], "int32"),
+    "pl": ("sbuf", [128, 1], "int32"),
+    "pif": ("sbuf", [128, 1], "float32"), "pgf": ("sbuf", [128, 1], "float32"), "pff": ("sbuf", [128, 1], "float32"),
+    "pbf": ("sbuf", [128, 1], "float32"), "pwf": ("sbuf", [128, 1], "float32"),
+    "PH": ("sbuf", [128, 16 * 128], "float16"), "PB": ("sbuf", [128, 8 * 128], "bfloat16"),
+    "BDh": ("sbuf", [128, 128], "float16"), "BDb": ("sbuf", [128, 128], "bfloat16"), "WU": ("sbuf", [128, 128], "bfloat16"),
+    "o8": ("sbuf", [128, 32], "bfloat16"), "sel": ("sbuf", [128, 128], "float32"),
+    "oneh": ("sbuf", [128, 128], "float16"), "c16": ("sbuf", [128, 512], "float16"),
+    "tmi": ("sbuf", [128, 512], "int32"), "tmask": ("sbuf", [128, 512], "float16"),
+    "kmi": ("sbuf", [128, 64], "int32"), "Km": ("sbuf", [128, 64], "float32"), "Kb": ("sbuf", [128, 64], "float32"),
+    "rmi": ("sbuf", [128, 1024], "int32"), "rmask": ("sbuf", [128, 1024], "bfloat16"),
+    "eyi": ("sbuf", [128, 1024], "int32"), "eye": ("sbuf", [128, 1024], "bfloat16"),
+    "lbi": ("sbuf", [128, 64], "int32"), "lb1": ("sbuf", [128, 64], "float32"), "lb": ("sbuf", [128, 64], "float32"),
+    "lsi": ("sbuf", [128, 64], "int32"), "ani": ("sbuf", [128, 64], "int32"), "thi": ("sbuf", [128, 1], "int32"),
+    "anf": ("sbuf", [128, 65], "float32"),
+    "ylf": ("sbuf", [128, 64], "float32"), "yaf": ("sbuf", [128, 64], "float32"), "yzf": ("sbuf", [128, 64], "bfloat16"),
+}
+PS = ["pA0", "pA1", "pD0", "pD1", "pC", "pV", "pU", "pY"]
+for _n in PS:
+    SCRATCH[_n] = ("psum", [128, 512], "float32")
+for _r in range(RO):
+    SCRATCH["SA%d" % _r] = ("sbuf", [128, 192], "float16")
+    SCRATCH["LA%d" % _r] = ("sbuf", [128, 192], "float16")
+    SCRATCH["SB%d" % _r] = ("sbuf", [128, 128], "float32")
+    SCRATCH["LB%d" % _r] = ("sbuf", [128, 128], "float32")
+DM = ["d_ls", "d_an", "d_z", "d_th"] + ["d_x%d" % j for j in range(4)] + ["d_t%d" % k for k in range(1, NT)] + ["d_out"]
+SEMAPHORES = ["sV", "sS", "sP", "sG", "lo"] + DM + ["ra%d" % r for r in range(RO)] + ["rb%d" % r for r in range(RO)]
+MSGA = [((0, 48), 3), ((48, 96), 1), ((96, 144), 2), ((144, 192), 2)]
+MSGB = [((0, 32), 3), ((32, 64), 1), ((64, 96), 2), ((96, 128), 1)]
+DMA_TABS, S_TABS, V_TABS = [1, 2, 3, 4], [5, 6], [7]
+
+
+def rank_program(g, core, T, topo):
+    rank = T.rank_of(core)
+    if rank is None:
+        return
+    ENG = {"V": g.vector, "S": g.scalar, "P": g.tensor, "G": g, "Y": g.sync}
+    known = {q: {} for q in ENG}
+    clock = {}
+    total = {}
+    acc = {}
+
+    def t(name, lo=0, hi=None, st=1, p0=0, p1=128, ps=1):
+        if hi is None:
+            hi = SCRATCH[name][1][1]
+        if p0 == 0 and p1 == 128 and ps == 1:
+            ap = T[name][:, lo:hi] if st == 1 else T[name][:, lo:hi:st]
+        else:
+            ap = T[name][p0:p1, lo:hi] if ps == 1 else T[name][p0:p1:ps, lo:hi]
+        return (ap, [(name, lo, hi)])
+
+    def ind(win, off):
+        return (win[0].indirect(off[0]), win[1] + off[1])
+
+    def outside(ap):
+        return (ap, [])
+
+    def need(q, regs, isw):
+        own = "s" + q
+        out = {}
+        for name, lo, hi in regs:
+            ps = name in PS
+            for a, b, sem, val, w in acc.get(name, []):
+                over = a < hi and lo < b
+                if sem == own:
+                    hit = over and w and not isw
+                elif ps:
+                    hit = True
+                else:
+                    hit = over and (w or isw)
+                if hit and known[q].get(sem, 0) < val:
+                    out[sem] = max(out.get(sem, 0), val)
+        return out
+
+    def note(regs, sem, val, isw):
+        for name, lo, hi in regs:
+            lst = [e for e in acc.get(name, []) if not (e[0] >= lo and e[1] <= hi and e[2] == sem and (e[4] == isw))]
+            lst.append((lo, hi, sem, val, isw))
+            acc[name] = lst
+
+    def prepare(q, reads, writes):
+        w = {}
+        for regs, isw in ((reads, False), (writes, True)):
+            for s, v in need(q, regs, isw).items():
+                w[s] = max(w.get(s, 0), v)
+        for s in sorted(w):
+            if any(o != s and clock.get((o, w[o]), {}).get(s, 0) >= w[s] and known[q].get(o, 0) < w[o] for o in w):
+                continue
+            if known[q].get(s, 0) >= w[s]:
+                continue
+            ENG[q].wait_ge(T.sem[s], w[s])
+            k = known[q]
+            for a, b in clock.get((s, w[s]), {}).items():
+                k[a] = max(k.get(a, 0), b)
+            k[s] = max(k.get(s, 0), w[s])
+
+    def finish(q, ins, sem, n, reads, writes):
+        total[sem] = total.get(sem, 0) + n
+        ins.then_inc(T.sem[sem], n)
+        clock[(sem, total[sem])] = dict(known[q])
+        note(reads, sem, total[sem], False)
+        note(writes, sem, total[sem], True)
+
+    def op(q, fn, out, ins, *rest, **kw):
+        reads = []
+        for a in ins:
+            if isinstance(a, tuple):
+                reads = reads + a[1]
+        if "bias" in kw and isinstance(kw["bias"], tuple):
+            reads = reads + kw["bias"][1]
+            kw["bias"] = kw["bias"][0]
+        wr = out[1]
+        if len(wr) > 1:
+            reads = reads + wr[1:]
+            wr = wr[:1]
+        prepare(q, reads, wr)
+        i = fn(out[0], *([a[0] if isinstance(a, tuple) else a for a in ins] + list(rest)), **kw)
+        finish(q, i, "s" + q, 1, reads, wr)
+
+    def tt(out, a, b, o):
+        op("V", g.vector.tensor_tensor, out, [a, b, o])
+
+    def ts(out, a, s1, o1, s2=None, o2=None):
+        if o2 is None:
+            op("V", g.vector.tensor_scalar, out, [a, s1, None, o1])
+        else:
+            op("V", g.vector.tensor_scalar, out, [a, s1, s2, o1, o2])
+
+    def cp(out, a):
+        op("V", g.vector.tensor_copy, out, [a])
+
+    def act(out, a, f, **kw):
+        op("S", g.scalar.activation, out, [a, f], **kw)
+
+    def mm(out, l, r, start=True, stop=True):
+        op("P", g.tensor.matmul, out, [l, r, start, stop])
+
+    def dma(q, sem, out, a):
+        prepare(q, a[1], out[1])
+        i = ENG[q].dma_start(out[0], a[0])
+        finish(q, i, sem, 16, a[1], out[1])
+
+    for b in range(4):
+        s = 16 * ORD[b]
+        dma("S", "d_ls", t("lsi", 16 * b, 16 * b + 16), outside(T.ls[:, s:s + 16]))
+    for b in range(4):
+        s = 16 * ORD[b]
+        dma("S", "d_an", t("ani", 16 * b, 16 * b + 16, p1=8), outside(T.an[:, s:s + 16]))
+    dma("S", "d_th", t("thi", p1=8), outside(T.th[:, 0:1]))
+    for b in range(4):
+        s = 16 * ORD[b]
+        dma("S", "d_z", t("zb", 16 * b, 16 * b + 16), outside(T.z[:, s:s + 16]))
+    for j in range(4):
+        dma("Y", "d_x%d" % j, t("tab", 1024 * j, 1024 * j + 1024), outside(T.x[:, 1024 * j:1024 * j + 1024]))
+    for k in DMA_TABS:
+        lo, hi = 4096 * k, 4096 * k + 4096
+        for gg in range(8):
+            dma("Y", "d_t%d" % k, t("tab", lo, hi, p0=16 * gg + k, p1=16 * gg + 16), outside(T.x[16 * gg:16 * gg + 16 - k, :]))
+        for f in range(k):
+            dma("Y", "d_t%d" % k, t("tab", lo, hi, p0=f, p1=128, ps=16), outside(T.x[16 + f - k::16, :]))
+
+    def iota(out, pattern, base, cm):
+        op("G", g.iota, out, [], pattern, base, cm)
+
+    iota(t("pi"), [[0, 1]], 0, 1)
+    iota(t("J"), [[-1, 16]], 16, 1)
+    iota(t("mi"), [[1, 128]], 0, 0)
+    iota(t("tmi"), [[0, 4], [16, 8], [0, 16]], 0, 0)
+    iota(t("kmi"), [[16, 4], [-64, 16]], 960, 0)
+    iota(t("rmi"), [[0, 64], [1, 16]], 0, 0)
+    iota(t("eyi"), [[-1, 16], [0, 64]], 15, 0)
+    for b in range(4):
+        iota(t("lbi", 16 * b, 16 * b + 16), [[64, 16]], 1024 * ORD[b] - 100000, 0)
+    SH, AND = Op.arith_shift_right, Op.bitwise_and
+    ts(t("pj"), t("pi"), 15, AND)
+    ts(t("pk"), t("pi"), 4, SH)
+    ts(t("pl"), t("pi"), 112, AND)
+    ts(t("J2"), t("J"), 15, AND)
+    cp(t("pif"), t("pi"))
+    cp(t("pff"), t("pj"))
+    cp(t("pgf"), t("pk"))
+    cp(t("pbf"), t("pl"))
+    cp(t("mh"), t("mi"))
+    ts(t("ms"), t("mi"), 4, SH)
+    ts(t("tg"), t("J2"), t("pbf"), Op.add)
+    ts(t("sel", p1=8), t("ms", p1=8), t("pif", p1=8), Op.is_equal)
+    for k in range(16):
+        ts(t("PH", 128 * k, 128 * k + 128), t("mh"), t("tg", k, k + 1), Op.is_equal)
+    ts(t("oneh"), t("mh"), 0.0, Op.mult, 1.0, Op.add)
+    ts(t("c16", p1=32), t("tmi", p1=32), 0.0, Op.mult, 2016.0, Op.add)
+    ts(t("L16"), t("lsi"), -2048.0, Op.add)
+    ts(t("B"), t("lsi"), 32.0, Op.add)
+    cp(t("anf", 0, 64, p1=8), t("ani", p1=8))
+    cp(t("anf", 64, 65, p1=8), t("thi", p1=8))
+    mm(t("pU", 0, 65), t("sel", p1=8), t("anf", p1=8))
+    ts(t("C0"), t("pU", 0, 64), 32.0, Op.mult, 1024.0 - 8388608.0, Op.add)
+    ts(t("nT"), t("pU", 64, 65), -1.0, Op.mult, 1785.0, Op.add)
+    for k in range(8, 16):
+        ts(t("PB", 128 * (k - 8), 128 * (k - 8) + 128), t("mh"), t("tg", k, k + 1), Op.is_equal)
+
+    def perm_b(k):
+        return t("PB", 128 * (k - 8), 128 * (k - 8) + 128)
+
+    def names_pe(h):
+        pa = "pA%d" % h
+        mm(t(pa), t("oneh", p1=1), t("c16", p1=1), True, False)
+        for k in range(8):
+            mm(t(pa, 64 * k, 64 * k + 64), t("PH", 128 * (8 * h + k), 128 * (8 * h + k) + 128), t("L16"), False, k == 7)
+
+    def names_v(h, C):
+        pa = "pA%d" % h
+        for k in range(8):
+            sl = t(pa, 64 * k, 64 * k + 64)
+            tt(sl, sl, t("B"), Op.mult)
+        for k in range(8):
+            c = (15 - 8 * h - k) * 64
+            tt(t("W", c, c + 64), t(pa, 64 * k, 64 * k + 64), C, Op.add)
+        c = 512 * (1 - h)
+        ts(t("E", c, c + 512), t("W", c, c + 512), 5, SH, 4095, AND)
+        for k in range(8):
+            c = (15 - 8 * h - k) * 64
+            ts(t("off%d" % h, k, 512, 8), t("E", c, c + 64), 4096.0 * k, Op.add)
+
+    names_pe(0)
+    names_pe(1)
+    def turn(k, j, bank, q):
+        mm(t(bank), perm_b(16 - k), t("tab", 512 * j, 512 * j + 512))
+        o = t("tab", 4096 * k + 512 * j, 4096 * k + 512 * j + 512)
+        if q == "S":
+            act(o, t(bank), Act.Copy)
+        else:
+            cp(o, t(bank))
+    names_v(0, t("C0"))
+    names_v(1, t("C0"))
+    mm(t("pV", 64, 128), perm_b(8), t("zb"))
+    act(t("z8"), t("pV", 64, 128), Act.Copy)
+    act(t("zh"), t("zb"), Act.Copy, scale=0.5, bias=-0.25)
+    seq_s = [(k, j) for k in S_TABS for j in range(8)]
+    seq_v = [(k, j) for k in V_TABS for j in range(8)]
+    ts(t("o8", 0, 8), t("mh", 0, 8), t("pgf"), Op.is_equal)
+    ts(t("o8", 8, 16), t("mh", 0, 8), t("pgf"), Op.is_equal, 2.0, Op.mult)
+    ts(t("o8", 16, 24), t("mh", 0, 8), t("pgf"), Op.is_equal, -1.0, Op.mult)
+    ts(t("o8", 24, 32), t("mh", 0, 8), t("pgf"), Op.is_equal, 1024.0, Op.mult)
+    ts(t("tmask"), t("tmi"), t("pif"), Op.is_equal)
+    ts(t("thr"), t("tmask"), t("nT"), Op.mult)
+    n = max(len(seq_s), len(seq_v))
+    for i in range(n):
+        if i < len(seq_s):
+            turn(seq_s[i][0], seq_s[i][1], ("pD0", "pD1")[i % 2], "S")
+        if i < len(seq_v):
+            turn(seq_v[i][0], seq_v[i][1], ("pY", "pU")[i % 2], "V")
+
+    def late_constants():
+        ts(t("BDh"), t("ms"), t("pgf"), Op.is_equal)
+        ts(t("BDb"), t("ms"), t("pgf"), Op.is_equal)
+        ts(t("pwf"), t("pff"), 2.0, Op.mult, 1.0, Op.add)
+        ts(t("WU"), t("ms"), t("pgf"), Op.is_equal, t("pwf"), Op.mult)
+        ts(t("Km"), t("kmi"), t("pff"), Op.add)
+        ts(t("Kb"), t("Km"), 16384.0, Op.add)
+        ts(t("rmask"), t("rmi"), 0.5, Op.is_gt)
+        ts(t("eye"), t("eyi"), t("pff"), Op.is_equal)
+        ts(t("lb1"), t("rmi", 0, 64), t("pff"), Op.is_equal, 100000.0, Op.mult)
+        tt(t("lb"), t("lb1"), t("lbi"), Op.add)
+        for r in range(RO):
+            ts(t("SA%d" % r, 80, 96), t("oneh", 0, 16), 0.0, Op.mult)
+            ts(t("SA%d" % r, 176, 192), t("oneh", 0, 16), 0.0, Op.mult)
+
+    def send(name, land, msg, sem):
+        dsts = [T.cores[(rank + d) % 4] for _, d in msg]
+        prepare("G", t(name)[1], [])
+        tr = []
+        for j, ((lo, hi), d) in enumerate(msg):
+            dst = dsts[j]
+            rid, pid, _ = topo.addr(dst)
+            e = topo.engines(core, dst)
+            n = 8 // len(msg)
+            m = 0
+            for x in e[n * j:n * j + n]:
+                m |= 1 << x
+            tr.append(RemoteDMATransfer(dst_ids=[DstId(rid=rid, pnc=pid)], dma_engine_mask=m, remote_sem=T.sem[sem],
+                                        src=T[name][:, lo:hi], dst=T[land][:, lo:hi]))
+        g.remote_dma_fused(tr, local_sem=T.sem.lo)
+        total["lo"] = total.get("lo", 0) + 8
+        total[sem] = 8
+        note([(land, 0, hi)], sem, 8, True)
+
+    def dbank(k1, q):
+        b, l = q // 16, q % 16
+        if k1 == 0:
+            return "pD0", 128 * b + l
+        if b < 3:
+            return "pD1", 128 * b + l
+        return "pA0", l
+
+    def gathers(r):
+        chunks = [(k1, q) for k1 in range(2) for q in range(64)]
+        ts_, tv_ = 0.0, V_LATE[r]
+        plan = []
+        for c in chunks:
+            if ts_ + S_T <= tv_ + V_T + 0.0:
+                ts_ += S_T
+                plan.append("S")
+            else:
+                tv_ += V_T
+                plan.append("V")
+        left = {"pD0": 0, "pD1": 0, "pA0": 0}
+        for c, e in zip(chunks, plan):
+            left[dbank(*c)[0]] += 1 if e == "S" else 2
+        for bank, w in (("pD0", 512), ("pD1", 384), ("pA0", 128)):
+            mm(t(bank, 0, w), t("oneh"), t("thr", 0, w), True, False)
+
+        def dist(c, src, lo, w):
+            bank, col = dbank(*c)
+            left[bank] -= 1
+            mm(t(bank, col, col + 113, 16), t(src, lo, lo + 128), t("o8", w, w + 8), False, left[bank] == 0)
+
+        ns, nv, vdone = [0], [0], [0]
+        pend_s, pend_v = [], []
+
+        def flush_s():
+            for c, lo in reversed(pend_s):
+                dist(c, "sd", lo, 0)
+            pend_s.clear()
+
+        def flush_v():
+            if not pend_v:
+                return
+            a, b = pend_v[0][1], pend_v[-1][1] + 128
+            ts(t("vr", a, b), t("vd", a, b), 0.0, Op.max)
+            for c, lo in reversed(pend_v):
+                dist(c, "vr", lo, 8)
+                dist(c, "vd", lo, 16)
+            pend_v.clear()
+
+        def compare(bank, w, out, lo):
+            ts(t(out, lo, lo + w), t(bank, 0, w), 1785.0, Op.is_lt)
+
+        def count(k1, b):
+            mm(t("pC", 16 * b + 8 * k1, 16 * b + 8 * k1 + 8), t("cmp%d" % k1, 128 * b, 128 * b + 128), t("o8", 24, 32))
+
+        todo = {"pD0": ("pD0", 512, "cmp0", 0), "pD1": ("pD1", 384, "cmp1", 0), "pA0": ("pA0", 128, "cmp1", 384)}
+        lag = []
+        for i, (c, e) in enumerate(zip(chunks, plan)):
+            k1, q = c
+            src = ind(t("tab"), t("off%d" % k1, 8 * q, 8 * q + 8))
+            zc = t("z8" if k1 else "zb", q, q + 1)
+            if e == "S":
+                lo = 128 * ns[0]
+                ns[0] += 1
+                act(t("sd", lo, lo + 128), src, Act.Abs, bias=zc, scale=-1.0)
+                pend_s.append((c, lo))
+            else:
+                lo = 128 * nv[0]
+                nv[0] += 1
+                ts(t("vd", lo, lo + 128), src, zc, Op.subtract)
+                pend_v.append((c, lo))
+            last = i + 1 == len(chunks) or dbank(*chunks[i + 1])[0] != dbank(*c)[0]
+            near = len(chunks) - i <= 16
+            if last:
+                flush_v()
+                flush_s()
+                lag.append((dbank(*c)[0], i + 6))
+            else:
+                if len(pend_s) >= (2 if near else 4):
+                    flush_s()
+                if len(pend_v) >= (3 if near else 8):
+                    flush_v()
+            while lag and (lag[0][1] <= i and e == "V" or i + 1 == len(chunks)):
+                compare(*todo[lag.pop(0)[0]])
+            if i == 60 and r == 0:
+                late_constants()
+        for b in range(4):
+            count(0, b)
+            count(1, b)
+
+    def tail(r):
+        sa, sb = "SA%d" % r, "SB%d" % r
+        tt(t("En", 0, 64), t("pC", 0, 64), t("Km"), Op.add)
+        tt(t("En", 64, 128), t("Kb"), t("pC", 0, 64), Op.subtract)
+        op("V", g.vector.tensor_tensor_scan, t("Sc"), [t("rmask", 0, 128), t("En"), 0.0, Op.mult, Op.max])
+        cp(t("KI"), t("Sc", 15, 128, 16))
+        ts(t("KJ"), t("KI"), 1023, AND)
+        cp(t("koff"), t("KJ"))
+        cp(t("EtU"), ind(t("E"), t("koff")))
+        act(t("OO"), ind(t("eye"), t("koff")), Act.Copy)
+        c = S_BEST
+        act(t("G", 0, 16 * c), ind(t("tab", 0, 4096), t("EtU", 0, c)), Act.Copy, scale=0.5)
+        ts(t("hot"), t("Sc", 15, 64, 16), 9216.0, Op.is_ge)
+        for b in range(4):
+            mm(t("pU", 64, 65), t("BDb"), t("hot", b, b + 1), b == 0, b == 3)
+        if c < 64:
+            ts(t("G", 16 * c, 1024), ind(t("tab", 0, 4096), t("EtU", c, 64)), 0.5, Op.mult)
+        ts(t("Eb"), t("EtU", 64, 128), -2048.0, Op.add)
+        tt(t("Q"), t("Eb"), t("OO", 0, 64), Op.mult)
+        mm(t("pV", 0, 64), t("BDh"), t("Q"))
+        ts(t(sa, 32, 80), t("EtU", 0, 48), -2048.0, Op.add)
+        ts(t(sa, 96, 112), t("EtU", 48, 64), -2048.0, Op.add)
+        for dst, lo, q, n in (("Lc", 0, 0, 16), (sa, 112, 16, 32), (sa, 16, 48, 16)):
+            ts(t(dst, lo, lo + n), t("OO", 64 + q, 64 + q + n), -1.0, Op.mult, 1.0, Op.add)
+        for dst, lo, q, n in (("Lc", 16, 0, 16), (sa, 144, 16, 32), (sa, 0, 48, 16)):
+            tt(t(dst, lo, lo + n), t("pV", q, q + n), t("OO", 64 + q, 64 + q + n), Op.mult)
+        send(sa, "LA%d" % r, MSGA, "ra%d" % r)
+        if r + 1 < RO:
+            cp(t("Ai"), t("pU", 64, 65))
+            ts(t("Aj"), t("Ai"), 31, AND)
+            ts(t("ncol"), t("Aj"), -1.0, Op.mult, t("nT"), Op.add)
+            ts(t("thr"), t("tmask"), t("ncol"), Op.mult)
+        act(t("kA"), t("pU", 64, 65), Act.Copy, scale=32.0, bias=65536.0 + 1024.0 - 8388608.0)
+        op("V", g.vector.tensor_tensor_scan, t("Ms"), [t("rmask"), t("G"), 0.0, Op.mult, Op.max])
+        tt(t("Yi"), t("Ms", 15, 1024, 16), t("zh"), Op.add)
+        cp(t("Yb"), t("Yi"))
+        mm(t("pU", 0, 64), t("WU"), t("Yb"))
+        tt(t("dz"), t("Ms", 15, 1024, 16), t("zh"), Op.subtract)
+        for lo, q, n in ((0, 0, 16), (96, 16, 32), (80, 48, 16)):
+            act(t(sb, lo, lo + n), t("dz", q, q + n), Act.Abs, scale=2.0, bias=t("mhalf"))
+        cp(t("si"), t("pU", 0, 64))
+        ts(t("ui"), t("si"), 4095, AND)
+        ts(t("u1"), t("ui"), -2048.0, Op.add)
+        ts(t("u2"), t("ui"), 3232.0, Op.add)
+        tt(t("Wc"), t("u1"), t("u2"), Op.mult)
+        ts(t("Wd"), t("Wc"), 0x1FFE0, AND)
+        ts(t(sb, 16, 80), t("Wd"), t("kA"), Op.add)
+        send(sb, "LB%d" % r, MSGB, "rb%d" % r)
+        if r + 1 < RO:
+            for k in range(1, NT):
+                mm(t("pY", 64 * k, 64 * k + 64), perm_b(16 - k), t("Yb"))
+            act(t("Yr", 64, 512), t("pY", 64, 512), Act.Copy)
+        ts(t("w6"), t("si"), 63, AND)
+        tt(t("wv"), t("w6"), t("lb"), Op.add)
+        op("V", g.vector.tensor_tensor_scan, t("ws"), [t("rmask", 0, 64), t("wv"), 0.0, Op.mult, Op.max])
+        cp(t("woff"), t("ws", 15, 64, 16))
+        cp(ind(t("tab", 0, 4096), t("woff")), t("Yb"))
+        if r + 1 < RO:
+            for k in range(1, NT):
+                cp(ind(t("tab", 4096 * k, 4096 * k + 4096), t("woff")), t("Yr", 64 * k, 64 * k + 64))
+        else:
+            dma("Y", "d_out", outside(T.yx[:, :]), t("tab", 0, 4096))
+
+    def receive(r):
+        la, lb = "LA%d" % r, "LB%d" % r
+        for l, n, nmn, nmlo, rmlo, q in ((32, 16, "Lc", 0, 16, 0), (48, 32, la, 112, 144, 16), (96, 16, la, 16, 0, 48)):
+            tt(t("tm", q, q + n), t(la, l, l + n), t(nmn, nmlo, nmlo + n), Op.mult)
+        for l, n, nmn, nmlo, rmlo, q in ((32, 16, "Lc", 0, 16, 0), (48, 32, la, 112, 144, 16), (96, 16, la, 16, 0, 48)):
+            tt(t("L16", q, q + n), t("tm", q, q + n), t(nmn, rmlo, rmlo + n), Op.add)
+        if r + 1 < RO:
+            ts(t("B"), t("L16"), 2080.0, Op.add)
+            names_pe(0)
+            for lo, q, n in ((0, 0, 16), (96, 16, 32), (80, 48, 16)):
+                act(t("zb", q, q + n), t(lb, lo, lo + n), Act.Copy)
+            mm(t("pV", 64, 128), perm_b(8), t("zb"))
+            names_pe(1)
+            act(t("z8"), t("pV", 64, 128), Act.Copy)
+            act(t("zh"), t("zb"), Act.Copy, scale=0.5, bias=-0.25)
+            names_v(0, t(lb, 16, 80))
+            names_v(1, t(lb, 16, 80))
+        else:
+            for b in range(4):
+                s = 16 * ORD[b]
+                ts(t("ylf", s, s + 16), t("L16", 16 * b, 16 * b + 16), 2048.0, Op.add)
+            dma("Y", "d_out", outside(T.yl[:, :]), t("ylf"))
+            for lo, b in ((0, 0), (96, 1), (112, 2), (80, 3)):
+                s = 16 * ORD[b]
+                act(t("yzf", s, s + 16), t(lb, lo, lo + 16), Act.Copy)
+            dma("S", "d_out", outside(T.yz[:, :]), t("yzf"))
+            ts(t("Wc"), t(lb, 16, 80), 8388608.0 - 1024.0, Op.add)
+            ts(t("Wd"), t("Wc"), 5, SH, 4095, AND)
+            for b in range(4):
+                s = 16 * ORD[b]
+                cp(t("yaf", s, s + 16), t("Wd", 16 * b, 16 * b + 16))
+            dma("Y", "d_out", outside(T.ya[:, :]), t("yaf", p0=0, p1=128, ps=16))
+
+    ts(t("mhalf"), t("pif"), 0.0, Op.mult, -0.5, Op.add)
+    for r in range(RO):
+        gathers(r)
+        tail(r)
+        receive(r)
+    for s in sorted(total):
+        g.wait_ge(T.sem[s], total[s])
+
+
+SCRATCH["mhalf"] = ("sbuf", [128, 1], "float32")

@@ -5,8 +5,13 @@ RO = 4
 ORD = [2, 0, 3, 1]
 NT = 8
 S_T, V_T = 0.224, 0.262
-V_LATE = [0.0, 1.9, 1.9, 1.9]
-S_BEST = 48
+V_LATE = [1.0, 2.6, 2.6, 2.6]
+MERGE_AT = 7
+S_BEST = 54
+DMA_TABS = [1, 2, 3, 4]
+TURN_S = [(k, j) for k in (5, 6) for j in range(8)] + [(7, j) for j in range(4)]
+TURN_V = [(7, j) for j in range(4, 8)]
+TURN = "SSSSSSSSSS" + "SV" * 4 + "SSSSSS"
 
 SCRATCH = {
     "tab": ("sbuf", [128, NT * 4096], "bfloat16"),
@@ -28,7 +33,7 @@ SCRATCH = {
     "Eb": ("sbuf", [128, 64], "float32"), "Q": ("sbuf", [128, 64], "float16"),
     "G": ("sbuf", [128, 1024], "bfloat16"), "Ms": ("sbuf", [128, 1024], "bfloat16"),
     "Yi": ("sbuf", [128, 64], "int32"), "Yb": ("sbuf", [128, 64], "bfloat16"), "Yr": ("sbuf", [128, 512], "bfloat16"),
-    "dz": ("sbuf", [128, 64], "float32"),
+    "dz": ("sbuf", [128, 64], "float32"), "mhalf": ("sbuf", [128, 1], "float32"),
     "si": ("sbuf", [128, 64], "int32"), "ui": ("sbuf", [128, 64], "int32"), "u1": ("sbuf", [128, 64], "float32"),
     "u2": ("sbuf", [128, 64], "float32"), "Wc": ("sbuf", [128, 64], "int32"), "Wd": ("sbuf", [128, 64], "int32"),
     "w6": ("sbuf", [128, 64], "int32"), "wv": ("sbuf", [128, 64], "float32"), "ws": ("sbuf", [128, 64], "float32"),
@@ -66,7 +71,6 @@ DM = ["d_ls", "d_an", "d_z", "d_th"] + ["d_x%d" % j for j in range(4)] + ["d_t%d
 SEMAPHORES = ["sV", "sS", "sP", "sG", "lo"] + DM + ["ra%d" % r for r in range(RO)] + ["rb%d" % r for r in range(RO)]
 MSGA = [((0, 48), 3), ((48, 96), 1), ((96, 144), 2), ((144, 192), 2)]
 MSGB = [((0, 32), 3), ((32, 64), 1), ((64, 96), 2), ((96, 128), 1)]
-DMA_TABS, S_TABS, V_TABS = [1, 2, 3, 4], [5, 6], [7]
 
 
 def rank_program(g, core, T, topo):
@@ -168,14 +172,17 @@ def rank_program(g, core, T, topo):
     def cp(out, a):
         op("V", g.vector.tensor_copy, out, [a])
 
+    def segmax(out, mask, a):
+        op("V", g.vector.tensor_tensor_scan, out, [mask, a, 0.0, Op.mult, Op.max])
+
     def act(out, a, f, **kw):
         op("S", g.scalar.activation, out, [a, f], **kw)
 
     def mm(out, l, r, start=True, stop=True):
         op("P", g.tensor.matmul, out, [l, r, start, stop])
 
-    def dma(q, sem, out, a):
-        prepare(q, a[1], out[1])
+    def dma(q, sem, out, a, fresh=False):
+        prepare(q, a[1], [] if fresh else out[1])
         i = ENG[q].dma_start(out[0], a[0])
         finish(q, i, sem, 16, a[1], out[1])
 
@@ -194,9 +201,9 @@ def rank_program(g, core, T, topo):
     for k in DMA_TABS:
         lo, hi = 4096 * k, 4096 * k + 4096
         for gg in range(8):
-            dma("Y", "d_t%d" % k, t("tab", lo, hi, p0=16 * gg + k, p1=16 * gg + 16), outside(T.x[16 * gg:16 * gg + 16 - k, :]))
+            dma("Y", "d_t%d" % k, t("tab", lo, hi, p0=16 * gg + k, p1=16 * gg + 16), outside(T.x[16 * gg:16 * gg + 16 - k, :]), True)
         for f in range(k):
-            dma("Y", "d_t%d" % k, t("tab", lo, hi, p0=f, p1=128, ps=16), outside(T.x[16 + f - k::16, :]))
+            dma("Y", "d_t%d" % k, t("tab", lo, hi, p0=f, p1=128, ps=16), outside(T.x[16 + f - k::16, :]), True)
 
     def iota(out, pattern, base, cm):
         op("G", g.iota, out, [], pattern, base, cm)
@@ -246,11 +253,13 @@ def rank_program(g, core, T, topo):
         for k in range(8):
             mm(t(pa, 64 * k, 64 * k + 64), t("PH", 128 * (8 * h + k), 128 * (8 * h + k) + 128), t("L16"), False, k == 7)
 
+    def names_mul(h):
+        for k in range(8):
+            sl = t("pA%d" % h, 64 * k, 64 * k + 64)
+            tt(sl, sl, t("B"), Op.mult)
+
     def names_v(h, C):
         pa = "pA%d" % h
-        for k in range(8):
-            sl = t(pa, 64 * k, 64 * k + 64)
-            tt(sl, sl, t("B"), Op.mult)
         for k in range(8):
             c = (15 - 8 * h - k) * 64
             tt(t("W", c, c + 64), t(pa, 64 * k, 64 * k + 64), C, Op.add)
@@ -262,6 +271,7 @@ def rank_program(g, core, T, topo):
 
     names_pe(0)
     names_pe(1)
+
     def turn(k, j, bank, q):
         mm(t(bank), perm_b(16 - k), t("tab", 512 * j, 512 * j + 512))
         o = t("tab", 4096 * k + 512 * j, 4096 * k + 512 * j + 512)
@@ -269,27 +279,30 @@ def rank_program(g, core, T, topo):
             act(o, t(bank), Act.Copy)
         else:
             cp(o, t(bank))
+    names_mul(0)
+    names_mul(1)
     names_v(0, t("C0"))
     names_v(1, t("C0"))
     mm(t("pV", 64, 128), perm_b(8), t("zb"))
     act(t("z8"), t("pV", 64, 128), Act.Copy)
     act(t("zh"), t("zb"), Act.Copy, scale=0.5, bias=-0.25)
-    seq_s = [(k, j) for k in S_TABS for j in range(8)]
-    seq_v = [(k, j) for k in V_TABS for j in range(8)]
     ts(t("o8", 0, 8), t("mh", 0, 8), t("pgf"), Op.is_equal)
     ts(t("o8", 8, 16), t("mh", 0, 8), t("pgf"), Op.is_equal, 2.0, Op.mult)
     ts(t("o8", 16, 24), t("mh", 0, 8), t("pgf"), Op.is_equal, -1.0, Op.mult)
     ts(t("o8", 24, 32), t("mh", 0, 8), t("pgf"), Op.is_equal, 1024.0, Op.mult)
     ts(t("tmask"), t("tmi"), t("pif"), Op.is_equal)
     ts(t("thr"), t("tmask"), t("nT"), Op.mult)
-    n = max(len(seq_s), len(seq_v))
-    for i in range(n):
-        if i < len(seq_s):
-            turn(seq_s[i][0], seq_s[i][1], ("pD0", "pD1")[i % 2], "S")
-        if i < len(seq_v):
-            turn(seq_v[i][0], seq_v[i][1], ("pY", "pU")[i % 2], "V")
+    si, vi = 0, 0
+    for q in TURN:
+        if q == "S":
+            turn(TURN_S[si][0], TURN_S[si][1], ("pD0", "pD1")[si % 2], "S")
+            si += 1
+        else:
+            turn(TURN_V[vi][0], TURN_V[vi][1], ("pY", "pU")[vi % 2], "V")
+            vi += 1
 
     def late_constants():
+        ts(t("mhalf"), t("pif"), 0.0, Op.mult, -0.5, Op.add)
         ts(t("BDh"), t("ms"), t("pgf"), Op.is_equal)
         ts(t("BDb"), t("ms"), t("pgf"), Op.is_equal)
         ts(t("pwf"), t("pff"), 2.0, Op.mult, 1.0, Op.add)
@@ -305,11 +318,10 @@ def rank_program(g, core, T, topo):
             ts(t("SA%d" % r, 176, 192), t("oneh", 0, 16), 0.0, Op.mult)
 
     def send(name, land, msg, sem):
-        dsts = [T.cores[(rank + d) % 4] for _, d in msg]
         prepare("G", t(name)[1], [])
         tr = []
         for j, ((lo, hi), d) in enumerate(msg):
-            dst = dsts[j]
+            dst = T.cores[(rank + d) % 4]
             rid, pid, _ = topo.addr(dst)
             e = topo.engines(core, dst)
             n = 8 // len(msg)
@@ -336,7 +348,7 @@ def rank_program(g, core, T, topo):
         ts_, tv_ = 0.0, V_LATE[r]
         plan = []
         for c in chunks:
-            if ts_ + S_T <= tv_ + V_T + 0.0:
+            if ts_ + S_T <= tv_ + V_T:
                 ts_ += S_T
                 plan.append("S")
             else:
@@ -353,7 +365,7 @@ def rank_program(g, core, T, topo):
             left[bank] -= 1
             mm(t(bank, col, col + 113, 16), t(src, lo, lo + 128), t("o8", w, w + 8), False, left[bank] == 0)
 
-        ns, nv, vdone = [0], [0], [0]
+        ns, nv = [0], [0]
         pend_s, pend_v = [], []
 
         def flush_s():
@@ -398,7 +410,7 @@ def rank_program(g, core, T, topo):
             if last:
                 flush_v()
                 flush_s()
-                lag.append((dbank(*c)[0], i + 6))
+                lag.append((dbank(*c)[0], i + 24))
             else:
                 if len(pend_s) >= (2 if near else 4):
                     flush_s()
@@ -406,29 +418,43 @@ def rank_program(g, core, T, topo):
                     flush_v()
             while lag and (lag[0][1] <= i and e == "V" or i + 1 == len(chunks)):
                 compare(*todo[lag.pop(0)[0]])
-            if i == 60 and r == 0:
-                late_constants()
         for b in range(4):
             count(0, b)
             count(1, b)
+
+    PIECES = (("Lc", 0, 16, 32, 16, 0), ("A", 112, 144, 48, 32, 16), ("A", 16, 0, 96, 16, 48))
+
+    def merge(r):
+        la = "LA%d" % r
+        for src, nm, rm, l, n, q in PIECES:
+            tt(t("tm", q, q + n), t(la, l, l + n), t(la if src == "A" else src, nm, nm + n), Op.mult)
+        for src, nm, rm, l, n, q in PIECES:
+            tt(t("L16", q, q + n), t("tm", q, q + n), t(la if src == "A" else src, rm, rm + n), Op.add)
+        if r + 1 < RO:
+            ts(t("B"), t("L16"), 2080.0, Op.add)
+            names_pe(0)
+            names_pe(1)
 
     def tail(r):
         sa, sb = "SA%d" % r, "SB%d" % r
         tt(t("En", 0, 64), t("pC", 0, 64), t("Km"), Op.add)
         tt(t("En", 64, 128), t("Kb"), t("pC", 0, 64), Op.subtract)
-        op("V", g.vector.tensor_tensor_scan, t("Sc"), [t("rmask", 0, 128), t("En"), 0.0, Op.mult, Op.max])
+        segmax(t("Sc"), t("rmask", 0, 128), t("En"))
         cp(t("KI"), t("Sc", 15, 128, 16))
         ts(t("KJ"), t("KI"), 1023, AND)
         cp(t("koff"), t("KJ"))
-        cp(t("EtU"), ind(t("E"), t("koff")))
-        act(t("OO"), ind(t("eye"), t("koff")), Act.Copy)
+        act(t("OO", 0, 64), ind(t("eye"), t("koff", 0, 4)), Act.Copy)
+        cp(t("EtU", 0, 64), ind(t("E"), t("koff", 0, 4)))
         c = S_BEST
-        act(t("G", 0, 16 * c), ind(t("tab", 0, 4096), t("EtU", 0, c)), Act.Copy, scale=0.5)
+        for lo, hi in ((0, 32), (32, c)):
+            act(t("G", 16 * lo, 16 * hi), ind(t("tab", 0, 4096), t("EtU", lo, hi)), Act.Copy, scale=0.5)
         ts(t("hot"), t("Sc", 15, 64, 16), 9216.0, Op.is_ge)
         for b in range(4):
             mm(t("pU", 64, 65), t("BDb"), t("hot", b, b + 1), b == 0, b == 3)
         if c < 64:
             ts(t("G", 16 * c, 1024), ind(t("tab", 0, 4096), t("EtU", c, 64)), 0.5, Op.mult)
+        cp(t("EtU", 64, 128), ind(t("E"), t("koff", 4, 8)))
+        cp(t("OO", 64, 128), ind(t("eye"), t("koff", 4, 8)))
         ts(t("Eb"), t("EtU", 64, 128), -2048.0, Op.add)
         tt(t("Q"), t("Eb"), t("OO", 0, 64), Op.mult)
         mm(t("pV", 0, 64), t("BDh"), t("Q"))
@@ -439,13 +465,9 @@ def rank_program(g, core, T, topo):
         for dst, lo, q, n in (("Lc", 16, 0, 16), (sa, 144, 16, 32), (sa, 0, 48, 16)):
             tt(t(dst, lo, lo + n), t("pV", q, q + n), t("OO", 64 + q, 64 + q + n), Op.mult)
         send(sa, "LA%d" % r, MSGA, "ra%d" % r)
-        if r + 1 < RO:
-            cp(t("Ai"), t("pU", 64, 65))
-            ts(t("Aj"), t("Ai"), 31, AND)
-            ts(t("ncol"), t("Aj"), -1.0, Op.mult, t("nT"), Op.add)
-            ts(t("thr"), t("tmask"), t("ncol"), Op.mult)
         act(t("kA"), t("pU", 64, 65), Act.Copy, scale=32.0, bias=65536.0 + 1024.0 - 8388608.0)
-        op("V", g.vector.tensor_tensor_scan, t("Ms"), [t("rmask"), t("G"), 0.0, Op.mult, Op.max])
+        for lo in (0, 512):
+            segmax(t("Ms", lo, lo + 512), t("rmask", lo, lo + 512), t("G", lo, lo + 512))
         tt(t("Yi"), t("Ms", 15, 1024, 16), t("zh"), Op.add)
         cp(t("Yb"), t("Yi"))
         mm(t("pU", 0, 64), t("WU"), t("Yb"))
@@ -466,32 +488,37 @@ def rank_program(g, core, T, topo):
             act(t("Yr", 64, 512), t("pY", 64, 512), Act.Copy)
         ts(t("w6"), t("si"), 63, AND)
         tt(t("wv"), t("w6"), t("lb"), Op.add)
-        op("V", g.vector.tensor_tensor_scan, t("ws"), [t("rmask", 0, 64), t("wv"), 0.0, Op.mult, Op.max])
+        segmax(t("ws"), t("rmask", 0, 64), t("wv"))
         cp(t("woff"), t("ws", 15, 64, 16))
         cp(ind(t("tab", 0, 4096), t("woff")), t("Yb"))
         if r + 1 < RO:
             for k in range(1, NT):
+                if k == MERGE_AT:
+                    merge(r)
                 cp(ind(t("tab", 4096 * k, 4096 * k + 4096), t("woff")), t("Yr", 64 * k, 64 * k + 64))
+            names_mul(0)
+            names_mul(1)
         else:
+            merge(r)
             dma("Y", "d_out", outside(T.yx[:, :]), t("tab", 0, 4096))
 
+    def threshold():
+        cp(t("Ai"), t("pU", 64, 65))
+        ts(t("Aj"), t("Ai"), 31, AND)
+        ts(t("ncol"), t("Aj"), -1.0, Op.mult, t("nT"), Op.add)
+        ts(t("thr"), t("tmask"), t("ncol"), Op.mult)
+
     def receive(r):
-        la, lb = "LA%d" % r, "LB%d" % r
-        for l, n, nmn, nmlo, rmlo, q in ((32, 16, "Lc", 0, 16, 0), (48, 32, la, 112, 144, 16), (96, 16, la, 16, 0, 48)):
-            tt(t("tm", q, q + n), t(la, l, l + n), t(nmn, nmlo, nmlo + n), Op.mult)
-        for l, n, nmn, nmlo, rmlo, q in ((32, 16, "Lc", 0, 16, 0), (48, 32, la, 112, 144, 16), (96, 16, la, 16, 0, 48)):
-            tt(t("L16", q, q + n), t("tm", q, q + n), t(nmn, rmlo, rmlo + n), Op.add)
+        lb = "LB%d" % r
         if r + 1 < RO:
-            ts(t("B"), t("L16"), 2080.0, Op.add)
-            names_pe(0)
             for lo, q, n in ((0, 0, 16), (96, 16, 32), (80, 48, 16)):
                 act(t("zb", q, q + n), t(lb, lo, lo + n), Act.Copy)
             mm(t("pV", 64, 128), perm_b(8), t("zb"))
-            names_pe(1)
             act(t("z8"), t("pV", 64, 128), Act.Copy)
             act(t("zh"), t("zb"), Act.Copy, scale=0.5, bias=-0.25)
             names_v(0, t(lb, 16, 80))
             names_v(1, t(lb, 16, 80))
+            threshold()
         else:
             for b in range(4):
                 s = 16 * ORD[b]
@@ -508,13 +535,10 @@ def rank_program(g, core, T, topo):
                 cp(t("yaf", s, s + 16), t("Wd", 16 * b, 16 * b + 16))
             dma("Y", "d_out", outside(T.ya[:, :]), t("yaf", p0=0, p1=128, ps=16))
 
-    ts(t("mhalf"), t("pif"), 0.0, Op.mult, -0.5, Op.add)
+    late_constants()
     for r in range(RO):
         gathers(r)
         tail(r)
         receive(r)
     for s in sorted(total):
         g.wait_ge(T.sem[s], total[s])
-
-
-SCRATCH["mhalf"] = ("sbuf", [128, 1], "float32")

@@ -5,13 +5,12 @@ RO = 4
 ORD = [2, 0, 3, 1]
 NT = 8
 S_T, V_T = 0.224, 0.262
-V_LATE = [1.0, 2.6, 2.6, 2.6]
-MERGE_AT = 7
-S_BEST = 54
-DMA_TABS = [1, 2, 3, 4]
-TURN_S = [(k, j) for k in (5, 6) for j in range(8)] + [(7, j) for j in range(4)]
-TURN_V = [(7, j) for j in range(4, 8)]
-TURN = "SSSSSSSSSS" + "SV" * 4 + "SSSSSS"
+V_LATE = [2.0, 3.5, 3.5, 3.5]
+NH = [40, 5, 5, 5]
+NV = [14, 0, 0, 0]
+S_BEST = 58
+DMA_TABS = [1, 2, 4, 5, 6]
+TURN_S, TURN_V = 3, 7
 
 SCRATCH = {
     "tab": ("sbuf", [128, NT * 4096], "bfloat16"),
@@ -29,11 +28,10 @@ SCRATCH = {
     "En": ("sbuf", [128, 128], "float32"), "Sc": ("sbuf", [128, 128], "float32"),
     "hot": ("sbuf", [128, 4], "bfloat16"),
     "KI": ("sbuf", [128, 8], "int32"), "KJ": ("sbuf", [128, 8], "int32"), "koff": ("sbuf", [128, 8], "uint16"),
-    "EtU": ("sbuf", [128, 128], "uint16"), "OO": ("sbuf", [128, 128], "bfloat16"),
+    "EtU": ("sbuf", [128, 64], "uint16"), "OO": ("sbuf", [128, 128], "bfloat16"),
     "Eb": ("sbuf", [128, 64], "float32"), "Q": ("sbuf", [128, 64], "float16"),
     "G": ("sbuf", [128, 1024], "bfloat16"), "Ms": ("sbuf", [128, 1024], "bfloat16"),
     "Yi": ("sbuf", [128, 64], "int32"), "Yb": ("sbuf", [128, 64], "bfloat16"), "Yr": ("sbuf", [128, 512], "bfloat16"),
-    "dz": ("sbuf", [128, 64], "float32"), "mhalf": ("sbuf", [128, 1], "float32"),
     "si": ("sbuf", [128, 64], "int32"), "ui": ("sbuf", [128, 64], "int32"), "u1": ("sbuf", [128, 64], "float32"),
     "u2": ("sbuf", [128, 64], "float32"), "Wc": ("sbuf", [128, 64], "int32"), "Wd": ("sbuf", [128, 64], "int32"),
     "w6": ("sbuf", [128, 64], "int32"), "wv": ("sbuf", [128, 64], "float32"), "ws": ("sbuf", [128, 64], "float32"),
@@ -41,19 +39,20 @@ SCRATCH = {
     "tm": ("sbuf", [128, 64], "float16"),
     "Lc": ("sbuf", [128, 32], "float16"),
     "J": ("sbuf", [128, 16], "int32"), "J2": ("sbuf", [128, 16], "int32"), "tg": ("sbuf", [128, 16], "float32"),
-    "mi": ("sbuf", [128, 128], "int32"), "mh": ("sbuf", [128, 128], "float16"), "ms": ("sbuf", [128, 128], "int32"),
+    "mh": ("sbuf", [128, 128], "bfloat16"), "ms": ("sbuf", [128, 128], "bfloat16"), "lm": ("sbuf", [128, 64], "bfloat16"),
     "pi": ("sbuf", [128, 1], "int32"), "pj": ("sbuf", [128, 1], "int32"), "pk": ("sbuf", [128, 1], "int32"),
     "pl": ("sbuf", [128, 1], "int32"),
     "pif": ("sbuf", [128, 1], "float32"), "pgf": ("sbuf", [128, 1], "float32"), "pff": ("sbuf", [128, 1], "float32"),
     "pbf": ("sbuf", [128, 1], "float32"), "pwf": ("sbuf", [128, 1], "float32"),
     "PH": ("sbuf", [128, 16 * 128], "float16"), "PB": ("sbuf", [128, 8 * 128], "bfloat16"),
     "BDh": ("sbuf", [128, 128], "float16"), "BDb": ("sbuf", [128, 128], "bfloat16"), "WU": ("sbuf", [128, 128], "bfloat16"),
+    "I2": ("sbuf", [128, 128], "bfloat16"), "In": ("sbuf", [128, 128], "bfloat16"),
     "o8": ("sbuf", [128, 32], "bfloat16"), "sel": ("sbuf", [128, 128], "float32"),
     "oneh": ("sbuf", [128, 128], "float16"), "c16": ("sbuf", [128, 512], "float16"),
-    "tmi": ("sbuf", [128, 512], "int32"), "tmask": ("sbuf", [128, 512], "float16"),
+    "tmi": ("sbuf", [128, 512], "bfloat16"), "tmask": ("sbuf", [128, 512], "float16"),
     "kmi": ("sbuf", [128, 64], "int32"), "Km": ("sbuf", [128, 64], "float32"), "Kb": ("sbuf", [128, 64], "float32"),
-    "rmi": ("sbuf", [128, 1024], "int32"), "rmask": ("sbuf", [128, 1024], "bfloat16"),
-    "eyi": ("sbuf", [128, 1024], "int32"), "eye": ("sbuf", [128, 1024], "bfloat16"),
+    "rmask": ("sbuf", [128, 1024], "bfloat16"),
+    "eyi": ("sbuf", [128, 1024], "bfloat16"), "eye": ("sbuf", [128, 1024], "bfloat16"),
     "lbi": ("sbuf", [128, 64], "int32"), "lb1": ("sbuf", [128, 64], "float32"), "lb": ("sbuf", [128, 64], "float32"),
     "lsi": ("sbuf", [128, 64], "int32"), "ani": ("sbuf", [128, 64], "int32"), "thi": ("sbuf", [128, 1], "int32"),
     "anf": ("sbuf", [128, 65], "float32"),
@@ -63,14 +62,14 @@ PS = ["pA0", "pA1", "pD0", "pD1", "pC", "pV", "pU", "pY"]
 for _n in PS:
     SCRATCH[_n] = ("psum", [128, 512], "float32")
 for _r in range(RO):
-    SCRATCH["SA%d" % _r] = ("sbuf", [128, 192], "float16")
+    SCRATCH["SA%d" % _r] = ("sbuf", [128, 160], "float16")
     SCRATCH["LA%d" % _r] = ("sbuf", [128, 192], "float16")
     SCRATCH["SB%d" % _r] = ("sbuf", [128, 128], "float32")
     SCRATCH["LB%d" % _r] = ("sbuf", [128, 128], "float32")
-DM = ["d_ls", "d_an", "d_z", "d_th"] + ["d_x%d" % j for j in range(4)] + ["d_t%d" % k for k in range(1, NT)] + ["d_out"]
+DM = ["d_ls", "d_an", "d_z", "d_th"] + ["d_x%d" % j for j in range(4)] + ["d_t%d" % k for k in DMA_TABS] + ["d_out"]
 SEMAPHORES = ["sV", "sS", "sP", "sG", "lo"] + DM + ["ra%d" % r for r in range(RO)] + ["rb%d" % r for r in range(RO)]
-MSGA = [((0, 48), 3), ((48, 96), 1), ((96, 144), 2), ((144, 192), 2)]
-MSGB = [((0, 32), 3), ((32, 64), 1), ((64, 96), 2), ((96, 128), 1)]
+MSGA = [(0, 0, 48, 3), (48, 48, 48, 1), (80, 96, 48, 2), (112, 144, 48, 2)]
+MSGB = [(0, 0, 32, 3), (32, 32, 32, 1), (64, 64, 32, 2), (96, 96, 32, 1)]
 
 
 def rank_program(g, core, T, topo):
@@ -173,7 +172,7 @@ def rank_program(g, core, T, topo):
         op("V", g.vector.tensor_copy, out, [a])
 
     def segmax(out, mask, a):
-        op("V", g.vector.tensor_tensor_scan, out, [mask, a, 0.0, Op.mult, Op.max])
+        op("V", g.vector.tensor_tensor_scan, out, [mask, a, 0.0, Op.min, Op.max])
 
     def act(out, a, f, **kw):
         op("S", g.scalar.activation, out, [a, f], **kw)
@@ -205,16 +204,19 @@ def rank_program(g, core, T, topo):
         for f in range(k):
             dma("Y", "d_t%d" % k, t("tab", lo, hi, p0=f, p1=128, ps=16), outside(T.x[16 + f - k::16, :]), True)
 
-    def iota(out, pattern, base, cm):
-        op("G", g.iota, out, [], pattern, base, cm)
+    def iota(out, pattern, base, cm, **kw):
+        op("G", g.iota, out, [], pattern, base, cm, **kw)
 
+    SM = {"allow_small_or_imprecise_dtypes": True}
     iota(t("pi"), [[0, 1]], 0, 1)
     iota(t("J"), [[-1, 16]], 16, 1)
-    iota(t("mi"), [[1, 128]], 0, 0)
-    iota(t("tmi"), [[0, 4], [16, 8], [0, 16]], 0, 0)
+    iota(t("mh"), [[1, 128]], 0, 0, **SM)
+    iota(t("ms"), [[1, 8], [0, 16]], 0, 0, **SM)
+    iota(t("tmi"), [[0, 4], [16, 8], [0, 16]], 0, 0, **SM)
     iota(t("kmi"), [[16, 4], [-64, 16]], 960, 0)
-    iota(t("rmi"), [[0, 64], [1, 16]], 0, 0)
-    iota(t("eyi"), [[-1, 16], [0, 64]], 15, 0)
+    iota(t("lm"), [[0, 4], [1, 16]], 0, 0, **SM)
+    iota(t("eyi"), [[-1, 16], [0, 64]], 15, 0, **SM)
+    iota(t("rmask"), [[0, 64], [32767, 16]], 0, 0, **SM)
     for b in range(4):
         iota(t("lbi", 16 * b, 16 * b + 16), [[64, 16]], 1024 * ORD[b] - 100000, 0)
     SH, AND = Op.arith_shift_right, Op.bitwise_and
@@ -226,8 +228,6 @@ def rank_program(g, core, T, topo):
     cp(t("pff"), t("pj"))
     cp(t("pgf"), t("pk"))
     cp(t("pbf"), t("pl"))
-    cp(t("mh"), t("mi"))
-    ts(t("ms"), t("mi"), 4, SH)
     ts(t("tg"), t("J2"), t("pbf"), Op.add)
     ts(t("sel", p1=8), t("ms", p1=8), t("pif", p1=8), Op.is_equal)
     for k in range(16):
@@ -258,16 +258,22 @@ def rank_program(g, core, T, topo):
             sl = t("pA%d" % h, 64 * k, 64 * k + 64)
             tt(sl, sl, t("B"), Op.mult)
 
-    def names_v(h, C):
+    def off_w(h, k):
+        return (T["off%d" % h][:, k:512:8], [("off%d#%d" % (h, k // 4), 0, 512)])
+
+    def off_r(h, a, b):
+        return (T["off%d" % h][:, a:b], [("off%d#%d" % (h, p), 0, 512) for p in range(2) if a % 8 // 4 <= p <= (b - 1) % 8 // 4])
+
+    def names_v(h, C, ks=range(8)):
         pa = "pA%d" % h
-        for k in range(8):
+        for k in ks:
             c = (15 - 8 * h - k) * 64
             tt(t("W", c, c + 64), t(pa, 64 * k, 64 * k + 64), C, Op.add)
-        c = 512 * (1 - h)
-        ts(t("E", c, c + 512), t("W", c, c + 512), 5, SH, 4095, AND)
-        for k in range(8):
+        c, w = (15 - 8 * h - ks[-1]) * 64, 64 * len(ks)
+        ts(t("E", c, c + w), t("W", c, c + w), 5, SH, 4095, AND)
+        for k in ks:
             c = (15 - 8 * h - k) * 64
-            ts(t("off%d" % h, k, 512, 8), t("E", c, c + 64), 4096.0 * k, Op.add)
+            ts(off_w(h, k), t("E", c, c + 64), 4096.0 * k, Op.add)
 
     names_pe(0)
     names_pe(1)
@@ -292,35 +298,28 @@ def rank_program(g, core, T, topo):
     ts(t("o8", 24, 32), t("mh", 0, 8), t("pgf"), Op.is_equal, 1024.0, Op.mult)
     ts(t("tmask"), t("tmi"), t("pif"), Op.is_equal)
     ts(t("thr"), t("tmask"), t("nT"), Op.mult)
-    si, vi = 0, 0
-    for q in TURN:
-        if q == "S":
-            turn(TURN_S[si][0], TURN_S[si][1], ("pD0", "pD1")[si % 2], "S")
-            si += 1
-        else:
-            turn(TURN_V[vi][0], TURN_V[vi][1], ("pY", "pU")[vi % 2], "V")
-            vi += 1
+    for j in range(8):
+        turn(TURN_S, j, ("pD0", "pD1")[j % 2], "S")
+    for j in range(8):
+        turn(TURN_V, j, ("pY", "pU")[j % 2], "V")
 
     def late_constants():
-        ts(t("mhalf"), t("pif"), 0.0, Op.mult, -0.5, Op.add)
+        ts(t("I2"), t("mh"), t("pif"), Op.is_equal, 2.0, Op.mult)
+        ts(t("In"), t("mh"), t("pif"), Op.is_equal, -1.0, Op.mult)
         ts(t("BDh"), t("ms"), t("pgf"), Op.is_equal)
         ts(t("BDb"), t("ms"), t("pgf"), Op.is_equal)
         ts(t("pwf"), t("pff"), 2.0, Op.mult, 1.0, Op.add)
-        ts(t("WU"), t("ms"), t("pgf"), Op.is_equal, t("pwf"), Op.mult)
         ts(t("Km"), t("kmi"), t("pff"), Op.add)
+        ts(t("WU"), t("ms"), t("pgf"), Op.is_equal, t("pwf"), Op.mult)
+        ts(t("lb1"), t("lm"), t("pff"), Op.is_equal, 100000.0, Op.mult)
         ts(t("Kb"), t("Km"), 16384.0, Op.add)
-        ts(t("rmask"), t("rmi"), 0.5, Op.is_gt)
         ts(t("eye"), t("eyi"), t("pff"), Op.is_equal)
-        ts(t("lb1"), t("rmi", 0, 64), t("pff"), Op.is_equal, 100000.0, Op.mult)
         tt(t("lb"), t("lb1"), t("lbi"), Op.add)
-        for r in range(RO):
-            ts(t("SA%d" % r, 80, 96), t("oneh", 0, 16), 0.0, Op.mult)
-            ts(t("SA%d" % r, 176, 192), t("oneh", 0, 16), 0.0, Op.mult)
 
     def send(name, land, msg, sem):
         prepare("G", t(name)[1], [])
         tr = []
-        for j, ((lo, hi), d) in enumerate(msg):
+        for j, (lo, at, w, d) in enumerate(msg):
             dst = T.cores[(rank + d) % 4]
             rid, pid, _ = topo.addr(dst)
             e = topo.engines(core, dst)
@@ -329,11 +328,11 @@ def rank_program(g, core, T, topo):
             for x in e[n * j:n * j + n]:
                 m |= 1 << x
             tr.append(RemoteDMATransfer(dst_ids=[DstId(rid=rid, pnc=pid)], dma_engine_mask=m, remote_sem=T.sem[sem],
-                                        src=T[name][:, lo:hi], dst=T[land][:, lo:hi]))
+                                        src=T[name][:, lo:lo + w], dst=T[land][:, at:at + w]))
         g.remote_dma_fused(tr, local_sem=T.sem.lo)
         total["lo"] = total.get("lo", 0) + 8
         total[sem] = 8
-        note([(land, 0, hi)], sem, 8, True)
+        note([(land, 0, 4 * msg[0][2])], sem, 8, True)
 
     def dbank(k1, q):
         b, l = q // 16, q % 16
@@ -343,12 +342,23 @@ def rank_program(g, core, T, topo):
             return "pD1", 128 * b + l
         return "pA0", l
 
+    def begin(r):
+        for q in range(NH[r]):
+            act(t("sd", 128 * q, 128 * q + 64), ind(t("tab", 0, 4 * 4096), off_r(0, 8 * q, 8 * q + 4)), Act.Abs,
+                bias=t("zb", q, q + 1), scale=-1.0)
+
     def gathers(r):
         chunks = [(k1, q) for k1 in range(2) for q in range(64)]
         ts_, tv_ = 0.0, V_LATE[r]
         plan = []
         for c in chunks:
-            if ts_ + S_T <= tv_ + V_T:
+            if len(plan) < NH[r]:
+                ts_ += 0.145
+                plan.append("S")
+            elif len(plan) < NH[r] + NV[r]:
+                tv_ += 0.18
+                plan.append("V")
+            elif ts_ + S_T <= tv_ + V_T:
                 ts_ += S_T
                 plan.append("S")
             else:
@@ -373,15 +383,16 @@ def rank_program(g, core, T, topo):
                 dist(c, "sd", lo, 0)
             pend_s.clear()
 
-        def flush_v():
-            if not pend_v:
+        def flush_v(keep=0):
+            now = pend_v[:len(pend_v) - keep]
+            if not now:
                 return
-            a, b = pend_v[0][1], pend_v[-1][1] + 128
+            a, b = now[0][1], now[-1][1] + 128
             ts(t("vr", a, b), t("vd", a, b), 0.0, Op.max)
-            for c, lo in reversed(pend_v):
+            for c, lo in reversed(now):
                 dist(c, "vr", lo, 8)
                 dist(c, "vd", lo, 16)
-            pend_v.clear()
+            del pend_v[:len(now)]
 
         def compare(bank, w, out, lo):
             ts(t(out, lo, lo + w), t(bank, 0, w), 1785.0, Op.is_lt)
@@ -393,36 +404,43 @@ def rank_program(g, core, T, topo):
         lag = []
         for i, (c, e) in enumerate(zip(chunks, plan)):
             k1, q = c
-            src = ind(t("tab"), t("off%d" % k1, 8 * q, 8 * q + 8))
+            src = ind(t("tab"), off_r(k1, 8 * q, 8 * q + 8))
+            src2 = ind(t("tab"), off_r(k1, 8 * q + 4, 8 * q + 8))
             zc = t("z8" if k1 else "zb", q, q + 1)
             if e == "S":
                 lo = 128 * ns[0]
                 ns[0] += 1
-                act(t("sd", lo, lo + 128), src, Act.Abs, bias=zc, scale=-1.0)
+                if i < NH[r]:
+                    act(t("sd", lo + 64, lo + 128), src2, Act.Abs, bias=zc, scale=-1.0)
+                else:
+                    act(t("sd", lo, lo + 128), src, Act.Abs, bias=zc, scale=-1.0)
                 pend_s.append((c, lo))
             else:
                 lo = 128 * nv[0]
                 nv[0] += 1
-                ts(t("vd", lo, lo + 128), src, zc, Op.subtract)
+                if i < NH[r] + NV[r]:
+                    ts(t("vd", lo + 64, lo + 128), src2, zc, Op.subtract)
+                else:
+                    ts(t("vd", lo, lo + 128), src, zc, Op.subtract)
                 pend_v.append((c, lo))
             last = i + 1 == len(chunks) or dbank(*chunks[i + 1])[0] != dbank(*c)[0]
             near = len(chunks) - i <= 16
             if last:
                 flush_v()
                 flush_s()
-                lag.append((dbank(*c)[0], i + 24))
+                lag.append((dbank(*c)[0], i + (24 if k1 == 0 else 12)))
             else:
                 if len(pend_s) >= (2 if near else 4):
                     flush_s()
-                if len(pend_v) >= (3 if near else 8):
-                    flush_v()
+                if len(pend_v) >= (4 if near else 9):
+                    flush_v(1)
             while lag and (lag[0][1] <= i and e == "V" or i + 1 == len(chunks)):
                 compare(*todo[lag.pop(0)[0]])
         for b in range(4):
             count(0, b)
             count(1, b)
 
-    PIECES = (("Lc", 0, 16, 32, 16, 0), ("A", 112, 144, 48, 32, 16), ("A", 16, 0, 96, 16, 48))
+    PIECES = (("Lc", 0, 16, 32, 16, 0), ("A", 112, 160, 48, 32, 16), ("A", 16, 0, 96, 16, 48))
 
     def merge(r):
         la = "LA%d" % r
@@ -444,7 +462,7 @@ def rank_program(g, core, T, topo):
         ts(t("KJ"), t("KI"), 1023, AND)
         cp(t("koff"), t("KJ"))
         act(t("OO", 0, 64), ind(t("eye"), t("koff", 0, 4)), Act.Copy)
-        cp(t("EtU", 0, 64), ind(t("E"), t("koff", 0, 4)))
+        cp(t("EtU"), ind(t("E"), t("koff", 0, 4)))
         c = S_BEST
         for lo, hi in ((0, 32), (32, c)):
             act(t("G", 16 * lo, 16 * hi), ind(t("tab", 0, 4096), t("EtU", lo, hi)), Act.Copy, scale=0.5)
@@ -453,60 +471,51 @@ def rank_program(g, core, T, topo):
             mm(t("pU", 64, 65), t("BDb"), t("hot", b, b + 1), b == 0, b == 3)
         if c < 64:
             ts(t("G", 16 * c, 1024), ind(t("tab", 0, 4096), t("EtU", c, 64)), 0.5, Op.mult)
-        cp(t("EtU", 64, 128), ind(t("E"), t("koff", 4, 8)))
+        ts(t("Eb"), ind(t("E"), t("koff", 4, 8)), -2048.0, Op.add)
         cp(t("OO", 64, 128), ind(t("eye"), t("koff", 4, 8)))
-        ts(t("Eb"), t("EtU", 64, 128), -2048.0, Op.add)
         tt(t("Q"), t("Eb"), t("OO", 0, 64), Op.mult)
         mm(t("pV", 0, 64), t("BDh"), t("Q"))
-        ts(t(sa, 32, 80), t("EtU", 0, 48), -2048.0, Op.add)
-        ts(t(sa, 96, 112), t("EtU", 48, 64), -2048.0, Op.add)
-        for dst, lo, q, n in (("Lc", 0, 0, 16), (sa, 112, 16, 32), (sa, 16, 48, 16)):
+        ts(t(sa, 32, 96), t("EtU"), -2048.0, Op.add)
+        for dst, lo, q, n in (("Lc", 0, 0, 16), (sa, 96, 16, 32), (sa, 16, 48, 16)):
             ts(t(dst, lo, lo + n), t("OO", 64 + q, 64 + q + n), -1.0, Op.mult, 1.0, Op.add)
-        for dst, lo, q, n in (("Lc", 16, 0, 16), (sa, 144, 16, 32), (sa, 0, 48, 16)):
+        segmax(t("Ms", 0, 512), t("rmask", 0, 512), t("G", 0, 512))
+        for dst, lo, q, n in (("Lc", 16, 0, 16), (sa, 128, 16, 32), (sa, 0, 48, 16)):
             tt(t(dst, lo, lo + n), t("pV", q, q + n), t("OO", 64 + q, 64 + q + n), Op.mult)
         send(sa, "LA%d" % r, MSGA, "ra%d" % r)
         act(t("kA"), t("pU", 64, 65), Act.Copy, scale=32.0, bias=65536.0 + 1024.0 - 8388608.0)
-        for lo in (0, 512):
-            segmax(t("Ms", lo, lo + 512), t("rmask", lo, lo + 512), t("G", lo, lo + 512))
+        segmax(t("Ms", 512, 1024), t("rmask", 512, 1024), t("G", 512, 1024))
         tt(t("Yi"), t("Ms", 15, 1024, 16), t("zh"), Op.add)
         cp(t("Yb"), t("Yi"))
         mm(t("pU", 0, 64), t("WU"), t("Yb"))
-        tt(t("dz"), t("Ms", 15, 1024, 16), t("zh"), Op.subtract)
+        mm(t("pV", 128, 192), t("I2"), t("Ms", 15, 1024, 16), True, False)
+        mm(t("pV", 128, 192), t("In"), t("zb"), False, True)
         for lo, q, n in ((0, 0, 16), (96, 16, 32), (80, 48, 16)):
-            act(t(sb, lo, lo + n), t("dz", q, q + n), Act.Abs, scale=2.0, bias=t("mhalf"))
+            act(t(sb, lo, lo + n), t("pV", 128 + q, 128 + q + n), Act.Abs)
         cp(t("si"), t("pU", 0, 64))
         ts(t("ui"), t("si"), 4095, AND)
+        ts(t("w6"), t("si"), 63, AND)
         ts(t("u1"), t("ui"), -2048.0, Op.add)
         ts(t("u2"), t("ui"), 3232.0, Op.add)
+        tt(t("wv"), t("w6"), t("lb"), Op.add)
         tt(t("Wc"), t("u1"), t("u2"), Op.mult)
+        segmax(t("ws"), t("rmask", 0, 64), t("wv"))
         ts(t("Wd"), t("Wc"), 0x1FFE0, AND)
+        cp(t("woff"), t("ws", 15, 64, 16))
         ts(t(sb, 16, 80), t("Wd"), t("kA"), Op.add)
         send(sb, "LB%d" % r, MSGB, "rb%d" % r)
         if r + 1 < RO:
             for k in range(1, NT):
                 mm(t("pY", 64 * k, 64 * k + 64), perm_b(16 - k), t("Yb"))
             act(t("Yr", 64, 512), t("pY", 64, 512), Act.Copy)
-        ts(t("w6"), t("si"), 63, AND)
-        tt(t("wv"), t("w6"), t("lb"), Op.add)
-        segmax(t("ws"), t("rmask", 0, 64), t("wv"))
-        cp(t("woff"), t("ws", 15, 64, 16))
         cp(ind(t("tab", 0, 4096), t("woff")), t("Yb"))
         if r + 1 < RO:
             for k in range(1, NT):
-                if k == MERGE_AT:
-                    merge(r)
                 cp(ind(t("tab", 4096 * k, 4096 * k + 4096), t("woff")), t("Yr", 64 * k, 64 * k + 64))
+            merge(r)
             names_mul(0)
-            names_mul(1)
         else:
             merge(r)
             dma("Y", "d_out", outside(T.yx[:, :]), t("tab", 0, 4096))
-
-    def threshold():
-        cp(t("Ai"), t("pU", 64, 65))
-        ts(t("Aj"), t("Ai"), 31, AND)
-        ts(t("ncol"), t("Aj"), -1.0, Op.mult, t("nT"), Op.add)
-        ts(t("thr"), t("tmask"), t("ncol"), Op.mult)
 
     def receive(r):
         lb = "LB%d" % r
@@ -516,9 +525,15 @@ def rank_program(g, core, T, topo):
             mm(t("pV", 64, 128), perm_b(8), t("zb"))
             act(t("z8"), t("pV", 64, 128), Act.Copy)
             act(t("zh"), t("zb"), Act.Copy, scale=0.5, bias=-0.25)
-            names_v(0, t(lb, 16, 80))
+            names_v(0, t(lb, 16, 80), range(4))
+            begin(r + 1)
+            cp(t("Ai"), t("pU", 64, 65))
+            names_v(0, t(lb, 16, 80), range(4, 8))
+            ts(t("Aj"), t("Ai"), 31, AND)
+            names_mul(1)
+            ts(t("ncol"), t("Aj"), -1.0, Op.mult, t("nT"), Op.add)
             names_v(1, t(lb, 16, 80))
-            threshold()
+            ts(t("thr"), t("tmask"), t("ncol"), Op.mult)
         else:
             for b in range(4):
                 s = 16 * ORD[b]
@@ -535,7 +550,11 @@ def rank_program(g, core, T, topo):
                 cp(t("yaf", s, s + 16), t("Wd", 16 * b, 16 * b + 16))
             dma("Y", "d_out", outside(T.ya[:, :]), t("yaf", p0=0, p1=128, ps=16))
 
+    begin(0)
     late_constants()
+    for j in range(NV[0]):
+        q = NH[0] + j
+        ts(t("vd", 128 * j, 128 * j + 64), ind(t("tab", 0, 4 * 4096), off_r(0, 8 * q, 8 * q + 4)), t("zb", q, q + 1), Op.subtract)
     for r in range(RO):
         gathers(r)
         tail(r)

from concourse.bass import DstId, RemoteDMATransfer
from concourse.mybir import AluOpType as Op, ActivationFunctionType as Act

RO = 4
ORD = [2, 0, 3, 1]
NT = 8
S_T, V_T = 0.224, 0.262
V_LATE = [2.0, 3.5, 3.5, 3.5]
NH = [40, 5, 5, 5]
NV = [14, 0, 0, 0]
S_BEST = 58
DMA_TABS = [1, 2, 4, 5, 6]
TURN_S, TURN_V = 3, 7

SCRATCH = {
    "tab": ("sbuf", [128, NT * 4096], "bfloat16"),
    "sd": ("sbuf", [128, 112 * 128], "bfloat16"),
    "vd": ("sbuf", [128, 96 * 128], "bfloat16"),
    "vr": ("sbuf", [128, 96 * 128], "bfloat16"),
    "W": ("sbuf", [128, 1024], "int32"), "E": ("sbuf", [128, 1024], "int32"),
    "off0": ("sbuf", [128, 512], "uint16"), "off1": ("sbuf", [128, 512], "uint16"),
    "L16": ("sbuf", [128, 64], "float16"), "B": ("sbuf", [128, 64], "float32"),
    "C0": ("sbuf", [128, 64], "float32"),
    "zb": ("sbuf", [128, 64], "bfloat16"), "z8": ("sbuf", [128, 64], "bfloat16"), "zh": ("sbuf", [128, 64], "float32"),
    "thr": ("sbuf", [128, 512], "float16"), "nT": ("sbuf", [128, 1], "float32"), "ncol": ("sbuf", [128, 1], "float32"),
    "kA": ("sbuf", [128, 1], "float32"), "Ai": ("sbuf", [128, 1], "int32"), "Aj": ("sbuf", [128, 1], "int32"),
    "cmp0": ("sbuf", [128, 512], "bfloat16"), "cmp1": ("sbuf", [128, 512], "bfloat16"),
    "En": ("sbuf", [128, 128], "float32"), "Sc": ("sbuf", [128, 128], "float32"),
    "hot": ("sbuf", [128, 4], "bfloat16"),
    "KI": ("sbuf", [128, 8], "int32"), "KJ": ("sbuf", [128, 8], "int32"), "koff": ("sbuf", [128, 8], "uint16"),
    "EtU": ("sbuf", [128, 64], "uint16"), "OO": ("sbuf", [128, 128], "bfloat16"),
    "Eb": ("sbuf", [128, 64], "float32"), "Q": ("sbuf", [128, 64], "float16"),
    "G": ("sbuf", [128, 1024], "bfloat16"), "Ms": ("sbuf", [128, 1024], "bfloat16"),
    "Yi": ("sbuf", [128, 64], "int32"), "Yb": ("sbuf", [128, 64], "bfloat16"), "Yr": ("sbuf", [128, 512], "bfloat16"),
    "si": ("sbuf", [128, 64], "int32"), "ui": ("sbuf", [128, 64], "int32"), "u1": ("sbuf", [128, 64], "float32"),
    "u2": ("sbuf", [128, 64], "float32"), "Wc": ("sbuf", [128, 64], "int32"), "Wd": ("sbuf", [128, 64], "int32"),
    "w6": ("sbuf", [128, 64], "int32"), "wv": ("sbuf", [128, 64], "float32"), "ws": ("sbuf", [128, 64], "float32"),
    "woff": ("sbuf", [128, 4], "uint16"),
    "tm": ("sbuf", [128, 64], "float16"),
    "Lc": ("sbuf", [128, 32], "float16"),
    "J": ("sbuf", [128, 16], "int32"), "J2": ("sbuf", [128, 16], "int32"), "tg": ("sbuf", [128, 16], "float32"),
    "mh": ("sbuf", [128, 128], "bfloat16"), "ms": ("sbuf", [128, 128], "bfloat16"), "lm": ("sbuf", [128, 64], "bfloat16"),
    "pi": ("sbuf", [128, 1], "int32"), "pj": ("sbuf", [128, 1], "int32"), "pk": ("sbuf", [128, 1], "int32"),
    "pl": ("sbuf", [128, 1], "int32"),
    "pif": ("sbuf", [128, 1], "float32"), "pgf": ("sbuf", [128, 1], "float32"), "pff": ("sbuf", [128, 1], "float32"),
    "pbf": ("sbuf", [128, 1], "float32"), "pwf": ("sbuf", [128, 1], "float32"),
    "PH": ("sbuf", [128, 16 * 128], "float16"), "PB": ("sbuf", [128, 8 * 128], "bfloat16"),
    "BDh": ("sbuf", [128, 128], "float16"), "BDb": ("sbuf", [128, 128], "bfloat16"), "WU": ("sbuf", [128, 128], "bfloat16"),
    "I2": ("sbuf", [128, 128], "bfloat16"), "In": ("sbuf", [128, 128], "bfloat16"),
    "o8": ("sbuf", [128, 32], "bfloat16"), "sel": ("sbuf", [128, 128], "float32"),
    "oneh": ("sbuf", [128, 128], "float16"), "c16": ("sbuf", [128, 512], "float16"),
    "tmi": ("sbuf", [128, 512], "bfloat16"), "tmask": ("sbuf", [128, 512], "float16"),
    "kmi": ("sbuf", [128, 64], "int32"), "Km": ("sbuf", [128, 64], "float32"), "Kb": ("sbuf", [128, 64], "float32"),
    "rmask": ("sbuf", [128, 1024], "bfloat16"),
    "eyi": ("sbuf", [128, 1024], "bfloat16"), "eye": ("sbuf", [128, 1024], "bfloat16"),
    "lbi": ("sbuf", [128, 64], "int32"), "lb1": ("sbuf", [128, 64], "float32"), "lb": ("sbuf", [128, 64], "float32"),
    "lsi": ("sbuf", [128, 64], "int32"), "ani": ("sbuf", [128, 64], "int32"), "thi": ("sbuf", [128, 1], "int32"),
    "anf": ("sbuf", [128, 65], "float32"),
    "ylf": ("sbuf", [128, 64], "float32"), "yaf": ("sbuf", [128, 64], "float32"), "yzf": ("sbuf", [128, 64], "bfloat16"),
}
PS = ["pA0", "pA1", "pD0", "pD1", "pC", "pV", "pU", "pY"]
for _n in PS:
    SCRATCH[_n] = ("psum", [128, 512], "float32")
for _r in range(RO):
    SCRATCH["SA%d" % _r] = ("sbuf", [128, 160], "float16")
    SCRATCH["LA%d" % _r] = ("sbuf", [128, 192], "float16")
    SCRATCH["SB%d" % _r] = ("sbuf", [128, 128], "float32")
    SCRATCH["LB%d" % _r] = ("sbuf", [128, 128], "float32")
DM = ["d_ls", "d_an", "d_z", "d_th"] + ["d_x%d" % j for j in range(4)] + ["d_t%d" % k for k in DMA_TABS] + ["d_out"]
SEMAPHORES = ["sV", "sS", "sP", "sG", "lo"] + DM + ["ra%d" % r for r in range(RO)] + ["rb%d" % r for r in range(RO)]
MSGA = [(0, 0, 48, 3), (48, 48, 48, 1), (80, 96, 48, 2), (112, 144, 48, 2)]
MSGB = [(0, 0, 32, 3), (32, 32, 32, 1), (64, 64, 32, 2), (96, 96, 32, 1)]


def rank_program(g, core, T, topo):
    rank = T.rank_of(core)
    if rank is None:
        return
    ENG = {"V": g.vector, "S": g.scalar, "P": g.tensor, "G": g, "Y": g.sync}
    known = {q: {} for q in ENG}
    clock = {}
    total = {}
    acc = {}

    def t(name, lo=0, hi=None, st=1, p0=0, p1=128, ps=1):
        if hi is None:
            hi = SCRATCH[name][1][1]
        if p0 == 0 and p1 == 128 and ps == 1:
            ap = T[name][:, lo:hi] if st == 1 else T[name][:, lo:hi:st]
        else:
            ap = T[name][p0:p1, lo:hi] if ps == 1 else T[name][p0:p1:ps, lo:hi]
        return (ap, [(name, lo, hi)])

    def ind(win, off):
        return (win[0].indirect(off[0]), win[1] + off[1])

    def outside(ap):
        return (ap, [])

    def need(q, regs, isw):
        own = "s" + q
        out = {}
        for name, lo, hi in regs:
            ps = name in PS
            for a, b, sem, val, w in acc.get(name, []):
                over = a < hi and lo < b
                if sem == own:
                    hit = over and w and not isw
                elif ps:
                    hit = True
                else:
                    hit = over and (w or isw)
                if hit and known[q].get(sem, 0) < val:
                    out[sem] = max(out.get(sem, 0), val)
        return out

    def note(regs, sem, val, isw):
        for name, lo, hi in regs:
            lst = [e for e in acc.get(name, []) if not (e[0] >= lo and e[1] <= hi and e[2] == sem and (e[4] == isw))]
            lst.append((lo, hi, sem, val, isw))
            acc[name] = lst

    def prepare(q, reads, writes):
        w = {}
        for regs, isw in ((reads, False), (writes, True)):
            for s, v in need(q, regs, isw).items():
                w[s] = max(w.get(s, 0), v)
        for s in sorted(w):
            if any(o != s and clock.get((o, w[o]), {}).get(s, 0) >= w[s] and known[q].get(o, 0) < w[o] for o in w):
                continue
            if known[q].get(s, 0) >= w[s]:
                continue
            ENG[q].wait_ge(T.sem[s], w[s])
            k = known[q]
            for a, b in clock.get((s, w[s]), {}).items():
                k[a] = max(k.get(a, 0), b)
            k[s] = max(k.get(s, 0), w[s])

    def finish(q, ins, sem, n, reads, writes):
        total[sem] = total.get(sem, 0) + n
        ins.then_inc(T.sem[sem], n)
        clock[(sem, total[sem])] = dict(known[q])
        note(reads, sem, total[sem], False)
        note(writes, sem, total[sem], True)

    def op(q, fn, out, ins, *rest, **kw):
        reads = []
        for a in ins:
            if isinstance(a, tuple):
                reads = reads + a[1]
        if "bias" in kw and isinstance(kw["bias"], tuple):
            reads = reads + kw["bias"][1]
            kw["bias"] = kw["bias"][0]
        wr = out[1]
        if len(wr) > 1:
            reads = reads + wr[1:]
            wr = wr[:1]
        prepare(q, reads, wr)
        i = fn(out[0], *([a[0] if isinstance(a, tuple) else a for a in ins] + list(rest)), **kw)
        finish(q, i, "s" + q, 1, reads, wr)

    def tt(out, a, b, o):
        op("V", g.vector.tensor_tensor, out, [a, b, o])

    def ts(out, a, s1, o1, s2=None, o2=None):
        if o2 is None:
            op("V", g.vector.tensor_scalar, out, [a, s1, None, o1])
        else:
            op("V", g.vector.tensor_scalar, out, [a, s1, s2, o1, o2])

    def cp(out, a):
        op("V", g.vector.tensor_copy, out, [a])

    def segmax(out, mask, a):
        op("V", g.vector.tensor_tensor_scan, out, [mask, a, 0.0, Op.min, Op.max])

    def act(out, a, f, **kw):
        op("S", g.scalar.activation, out, [a, f], **kw)

    def mm(out, l, r, start=True, stop=True):
        op("P", g.tensor.matmul, out, [l, r, start, stop])

    def dma(q, sem, out, a, fresh=False):
        prepare(q, a[1], [] if fresh else out[1])
        i = ENG[q].dma_start(out[0], a[0])
        finish(q, i, sem, 16, a[1], out[1])

    for b in range(4):
        s = 16 * ORD[b]
        dma("S", "d_ls", t("lsi", 16 * b, 16 * b + 16), outside(T.ls[:, s:s + 16]))
    for b in range(4):
        s = 16 * ORD[b]
        dma("S", "d_an", t("ani", 16 * b, 16 * b + 16, p1=8), outside(T.an[:, s:s + 16]))
    dma("S", "d_th", t("thi", p1=8), outside(T.th[:, 0:1]))
    for b in range(4):
        s = 16 * ORD[b]
        dma("S", "d_z", t("zb", 16 * b, 16 * b + 16), outside(T.z[:, s:s + 16]))
    for j in range(4):
        dma("Y", "d_x%d" % j, t("tab", 1024 * j, 1024 * j + 1024), outside(T.x[:, 1024 * j:1024 * j + 1024]))
    for k in DMA_TABS:
        lo, hi = 4096 * k, 4096 * k + 4096
        for gg in range(8):
            dma("Y", "d_t%d" % k, t("tab", lo, hi, p0=16 * gg + k, p1=16 * gg + 16), outside(T.x[16 * gg:16 * gg + 16 - k, :]), True)
        for f in range(k):
            dma("Y", "d_t%d" % k, t("tab", lo, hi, p0=f, p1=128, ps=16), outside(T.x[16 + f - k::16, :]), True)

    def iota(out, pattern, base, cm, **kw):
        op("G", g.iota, out, [], pattern, base, cm, **kw)

    SM = {"allow_small_or_imprecise_dtypes": True}
    iota(t("pi"), [[0, 1]], 0, 1)
    iota(t("J"), [[-1, 16]], 16, 1)
    iota(t("mh"), [[1, 128]], 0, 0, **SM)
    iota(t("ms"), [[1, 8], [0, 16]], 0, 0, **SM)
    iota(t("tmi"), [[0, 4], [16, 8], [0, 16]], 0, 0, **SM)
    iota(t("kmi"), [[16, 4], [-64, 16]], 960, 0)
    iota(t("lm"), [[0, 4], [1, 16]], 0, 0, **SM)
    iota(t("eyi"), [[-1, 16], [0, 64]], 15, 0, **SM)
    iota(t("rmask"), [[0, 64], [32767, 16]], 0, 0, **SM)
    for b in range(4):
        iota(t("lbi", 16 * b, 16 * b + 16), [[64, 16]], 1024 * ORD[b] - 100000, 0)
    SH, AND = Op.arith_shift_right, Op.bitwise_and
    ts(t("pj"), t("pi"), 15, AND)
    ts(t("pk"), t("pi"), 4, SH)
    ts(t("pl"), t("pi"), 112, AND)
    ts(t("J2"), t("J"), 15, AND)
    cp(t("pif"), t("pi"))
    cp(t("pff"), t("pj"))
    cp(t("pgf"), t("pk"))
    cp(t("pbf"), t("pl"))
    ts(t("tg"), t("J2"), t("pbf"), Op.add)
    ts(t("sel", p1=8), t("ms", p1=8), t("pif", p1=8), Op.is_equal)
    for k in range(16):
        ts(t("PH", 128 * k, 128 * k + 128), t("mh"), t("tg", k, k + 1), Op.is_equal)
    ts(t("oneh"), t("mh"), 0.0, Op.mult, 1.0, Op.add)
    ts(t("c16", p1=32), t("tmi", p1=32), 0.0, Op.mult, 2016.0, Op.add)
    ts(t("L16"), t("lsi"), -2048.0, Op.add)
    ts(t("B"), t("lsi"), 32.0, Op.add)
    cp(t("anf", 0, 64, p1=8), t("ani", p1=8))
    cp(t("anf", 64, 65, p1=8), t("thi", p1=8))
    mm(t("pU", 0, 65), t("sel", p1=8), t("anf", p1=8))
    ts(t("C0"), t("pU", 0, 64), 32.0, Op.mult, 1024.0 - 8388608.0, Op.add)
    ts(t("nT"), t("pU", 64, 65), -1.0, Op.mult, 1785.0, Op.add)
    for k in range(8, 16):
        ts(t("PB", 128 * (k - 8), 128 * (k - 8) + 128), t("mh"), t("tg", k, k + 1), Op.is_equal)

    def perm_b(k):
        return t("PB", 128 * (k - 8), 128 * (k - 8) + 128)

    def names_pe(h):
        pa = "pA%d" % h
        mm(t(pa), t("oneh", p1=1), t("c16", p1=1), True, False)
        for k in range(8):
            mm(t(pa, 64 * k, 64 * k + 64), t("PH", 128 * (8 * h + k), 128 * (8 * h + k) + 128), t("L16"), False, k == 7)

    def names_mul(h):
        for k in range(8):
            sl = t("pA%d" % h, 64 * k, 64 * k + 64)
            tt(sl, sl, t("B"), Op.mult)

    def off_w(h, k):
        return (T["off%d" % h][:, k:512:8], [("off%d#%d" % (h, k // 4), 0, 512)])

    def off_r(h, a, b):
        return (T["off%d" % h][:, a:b], [("off%d#%d" % (h, p), 0, 512) for p in range(2) if a % 8 // 4 <= p <= (b - 1) % 8 // 4])

    def names_v(h, C, ks=range(8)):
        pa = "pA%d" % h
        for k in ks:
            c = (15 - 8 * h - k) * 64
            tt(t("W", c, c + 64), t(pa, 64 * k, 64 * k + 64), C, Op.add)
        c, w = (15 - 8 * h - ks[-1]) * 64, 64 * len(ks)
        ts(t("E", c, c + w), t("W", c, c + w), 5, SH, 4095, AND)
        for k in ks:
            c = (15 - 8 * h - k) * 64
            ts(off_w(h, k), t("E", c, c + 64), 4096.0 * k, Op.add)

    names_pe(0)
    names_pe(1)

    def turn(k, j, bank, q):
        mm(t(bank), perm_b(16 - k), t("tab", 512 * j, 512 * j + 512))
        o = t("tab", 4096 * k + 512 * j, 4096 * k + 512 * j + 512)
        if q == "S":
            act(o, t(bank), Act.Copy)
        else:
            cp(o, t(bank))
    names_mul(0)
    names_mul(1)
    names_v(0, t("C0"))
    names_v(1, t("C0"))
    mm(t("pV", 64, 128), perm_b(8), t("zb"))
    act(t("z8"), t("pV", 64, 128), Act.Copy)
    act(t("zh"), t("zb"), Act.Copy, scale=0.5, bias=-0.25)
    ts(t("o8", 0, 8), t("mh", 0, 8), t("pgf"), Op.is_equal)
    ts(t("o8", 8, 16), t("mh", 0, 8), t("pgf"), Op.is_equal, 2.0, Op.mult)
    ts(t("o8", 16, 24), t("mh", 0, 8), t("pgf"), Op.is_equal, -1.0, Op.mult)
    ts(t("o8", 24, 32), t("mh", 0, 8), t("pgf"), Op.is_equal, 1024.0, Op.mult)
    ts(t("tmask"), t("tmi"), t("pif"), Op.is_equal)
    ts(t("thr"), t("tmask"), t("nT"), Op.mult)
    for j in range(8):
        turn(TURN_S, j, ("pD0", "pD1")[j % 2], "S")
    for j in range(8):
        turn(TURN_V, j, ("pY", "pU")[j % 2], "V")

    def late_constants():
        ts(t("I2"), t("mh"), t("pif"), Op.is_equal, 2.0, Op.mult)
        ts(t("In"), t("mh"), t("pif"), Op.is_equal, -1.0, Op.mult)
        ts(t("BDh"), t("ms"), t("pgf"), Op.is_equal)
        ts(t("BDb"), t("ms"), t("pgf"), Op.is_equal)
        ts(t("pwf"), t("pff"), 2.0, Op.mult, 1.0, Op.add)
        ts(t("Km"), t("kmi"), t("pff"), Op.add)
        ts(t("WU"), t("ms"), t("pgf"), Op.is_equal, t("pwf"), Op.mult)
        ts(t("lb1"), t("lm"), t("pff"), Op.is_equal, 100000.0, Op.mult)
        ts(t("Kb"), t("Km"), 16384.0, Op.add)
        ts(t("eye"), t("eyi"), t("pff"), Op.is_equal)
        tt(t("lb"), t("lb1"), t("lbi"), Op.add)

    def send(name, land, msg, sem):
        prepare("G", t(name)[1], [])
        tr = []
        for j, (lo, at, w, d) in enumerate(msg):
            dst = T.cores[(rank + d) % 4]
            rid, pid, _ = topo.addr(dst)
            e = topo.engines(core, dst)
            n = 8 // len(msg)
            m = 0
            for x in e[n * j:n * j + n]:
                m |= 1 << x
            tr.append(RemoteDMATransfer(dst_ids=[DstId(rid=rid, pnc=pid)], dma_engine_mask=m, remote_sem=T.sem[sem],
                                        src=T[name][:, lo:lo + w], dst=T[land][:, at:at + w]))
        g.remote_dma_fused(tr, local_sem=T.sem.lo)
        total["lo"] = total.get("lo", 0) + 8
        total[sem] = 8
        note([(land, 0, 4 * msg[0][2])], sem, 8, True)

    def dbank(k1, q):
        b, l = q // 16, q % 16
        if k1 == 0:
            return "pD0", 128 * b + l
        if b < 3:
            return "pD1", 128 * b + l
        return "pA0", l

    def begin(r):
        for q in range(NH[r]):
            act(t("sd", 128 * q, 128 * q + 64), ind(t("tab", 0, 4 * 4096), off_r(0, 8 * q, 8 * q + 4)), Act.Abs,
                bias=t("zb", q, q + 1), scale=-1.0)

    def gathers(r):
        chunks = [(k1, q) for k1 in range(2) for q in range(64)]
        ts_, tv_ = 0.0, V_LATE[r]
        plan = []
        for c in chunks:
            if len(plan) < NH[r]:
                ts_ += 0.145
                plan.append("S")
            elif len(plan) < NH[r] + NV[r]:
                tv_ += 0.18
                plan.append("V")
            elif ts_ + S_T <= tv_ + V_T:
                ts_ += S_T
                plan.append("S")
            else:
                tv_ += V_T
                plan.append("V")
        left = {"pD0": 0, "pD1": 0, "pA0": 0}
        for c, e in zip(chunks, plan):
            left[dbank(*c)[0]] += 1 if e == "S" else 2
        for bank, w in (("pD0", 512), ("pD1", 384), ("pA0", 128)):
            mm(t(bank, 0, w), t("oneh"), t("thr", 0, w), True, False)

        def dist(c, src, lo, w):
            bank, col = dbank(*c)
            left[bank] -= 1
            mm(t(bank, col, col + 113, 16), t(src, lo, lo + 128), t("o8", w, w + 8), False, left[bank] == 0)

        ns, nv = [0], [0]
        pend_s, pend_v = [], []

        def flush_s():
            for c, lo in reversed(pend_s):
                dist(c, "sd", lo, 0)
            pend_s.clear()

        def flush_v(keep=0):
            now = pend_v[:len(pend_v) - keep]
            if not now:
                return
            a, b = now[0][1], now[-1][1] + 128
            ts(t("vr", a, b), t("vd", a, b), 0.0, Op.max)
            for c, lo in reversed(now):
                dist(c, "vr", lo, 8)
                dist(c, "vd", lo, 16)
            del pend_v[:len(now)]

        def compare(bank, w, out, lo):
            ts(t(out, lo, lo + w), t(bank, 0, w), 1785.0, Op.is_lt)

        def count(k1, b):
            mm(t("pC", 16 * b + 8 * k1, 16 * b + 8 * k1 + 8), t("cmp%d" % k1, 128 * b, 128 * b + 128), t("o8", 24, 32))

        todo = {"pD0": ("pD0", 512, "cmp0", 0), "pD1": ("pD1", 384, "cmp1", 0), "pA0": ("pA0", 128, "cmp1", 384)}
        lag = []
        for i, (c, e) in enumerate(zip(chunks, plan)):
            k1, q = c
            src = ind(t("tab"), off_r(k1, 8 * q, 8 * q + 8))
            src2 = ind(t("tab"), off_r(k1, 8 * q + 4, 8 * q + 8))
            zc = t("z8" if k1 else "zb", q, q + 1)
            if e == "S":
                lo = 128 * ns[0]
                ns[0] += 1
                if i < NH[r]:
                    act(t("sd", lo + 64, lo + 128), src2, Act.Abs, bias=zc, scale=-1.0)
                else:
                    act(t("sd", lo, lo + 128), src, Act.Abs, bias=zc, scale=-1.0)
                pend_s.append((c, lo))
            else:
                lo = 128 * nv[0]
                nv[0] += 1
                if i < NH[r] + NV[r]:
                    ts(t("vd", lo + 64, lo + 128), src2, zc, Op.subtract)
                else:
                    ts(t("vd", lo, lo + 128), src, zc, Op.subtract)
                pend_v.append((c, lo))
            last = i + 1 == len(chunks) or dbank(*chunks[i + 1])[0] != dbank(*c)[0]
            near = len(chunks) - i <= 16
            if last:
                flush_v()
                flush_s()
                lag.append((dbank(*c)[0], i + (24 if k1 == 0 else 12)))
            else:
                if len(pend_s) >= (2 if near else 4):
                    flush_s()
                if len(pend_v) >= (4 if near else 9):
                    flush_v(1)
            while lag and (lag[0][1] <= i and e == "V" or i + 1 == len(chunks)):
                compare(*todo[lag.pop(0)[0]])
        for b in range(4):
            count(0, b)
            count(1, b)

    PIECES = (("Lc", 0, 16, 32, 16, 0), ("A", 112, 160, 48, 32, 16), ("A", 16, 0, 96, 16, 48))

    def merge(r):
        la = "LA%d" % r
        for src, nm, rm, l, n, q in PIECES:
            tt(t("tm", q, q + n), t(la, l, l + n), t(la if src == "A" else src, nm, nm + n), Op.mult)
        for src, nm, rm, l, n, q in PIECES:
            tt(t("L16", q, q + n), t("tm", q, q + n), t(la if src == "A" else src, rm, rm + n), Op.add)
        if r + 1 < RO:
            ts(t("B"), t("L16"), 2080.0, Op.add)
            names_pe(0)
            names_pe(1)

    def tail(r):
        sa, sb = "SA%d" % r, "SB%d" % r
        tt(t("En", 0, 64), t("pC", 0, 64), t("Km"), Op.add)
        tt(t("En", 64, 128), t("Kb"), t("pC", 0, 64), Op.subtract)
        segmax(t("Sc"), t("rmask", 0, 128), t("En"))
        cp(t("KI"), t("Sc", 15, 128, 16))
        ts(t("KJ"), t("KI"), 1023, AND)
        cp(t("koff"), t("KJ"))
        act(t("OO", 0, 64), ind(t("eye"), t("koff", 0, 4)), Act.Copy)
        cp(t("EtU"), ind(t("E"), t("koff", 0, 4)))
        c = S_BEST
        for lo, hi in ((0, 32), (32, c)):
            act(t("G", 16 * lo, 16 * hi), ind(t("tab", 0, 4096), t("EtU", lo, hi)), Act.Copy, scale=0.5)
        ts(t("hot"), t("Sc", 15, 64, 16), 9216.0, Op.is_ge)
        for b in range(4):
            mm(t("pU", 64, 65), t("BDb"), t("hot", b, b + 1), b == 0, b == 3)
        if c < 64:
            ts(t("G", 16 * c, 1024), ind(t("tab", 0, 4096), t("EtU", c, 64)), 0.5, Op.mult)
        ts(t("Eb"), ind(t("E"), t("koff", 4, 8)), -2048.0, Op.add)
        cp(t("OO", 64, 128), ind(t("eye"), t("koff", 4, 8)))
        tt(t("Q"), t("Eb"), t("OO", 0, 64), Op.mult)
        mm(t("pV", 0, 64), t("BDh"), t("Q"))
        ts(t(sa, 32, 96), t("EtU"), -2048.0, Op.add)
        for dst, lo, q, n in (("Lc", 0, 0, 16), (sa, 96, 16, 32), (sa, 16, 48, 16)):
            ts(t(dst, lo, lo + n), t("OO", 64 + q, 64 + q + n), -1.0, Op.mult, 1.0, Op.add)
        segmax(t("Ms", 0, 512), t("rmask", 0, 512), t("G", 0, 512))
        for dst, lo, q, n in (("Lc", 16, 0, 16), (sa, 128, 16, 32), (sa, 0, 48, 16)):
            tt(t(dst, lo, lo + n), t("pV", q, q + n), t("OO", 64 + q, 64 + q + n), Op.mult)
        send(sa, "LA%d" % r, MSGA, "ra%d" % r)
        act(t("kA"), t("pU", 64, 65), Act.Copy, scale=32.0, bias=65536.0 + 1024.0 - 8388608.0)
        segmax(t("Ms", 512, 1024), t("rmask", 512, 1024), t("G", 512, 1024))
        tt(t("Yi"), t("Ms", 15, 1024, 16), t("zh"), Op.add)
        cp(t("Yb"), t("Yi"))
        mm(t("pU", 0, 64), t("WU"), t("Yb"))
        mm(t("pV", 128, 192), t("I2"), t("Ms", 15, 1024, 16), True, False)
        mm(t("pV", 128, 192), t("In"), t("zb"), False, True)
        for lo, q, n in ((0, 0, 16), (96, 16, 32), (80, 48, 16)):
            act(t(sb, lo, lo + n), t("pV", 128 + q, 128 + q + n), Act.Abs)
        cp(t("si"), t("pU", 0, 64))
        ts(t("ui"), t("si"), 4095, AND)
        ts(t("w6"), t("si"), 63, AND)
        ts(t("u1"), t("ui"), -2048.0, Op.add)
        ts(t("u2"), t("ui"), 3232.0, Op.add)
        tt(t("wv"), t("w6"), t("lb"), Op.add)
        tt(t("Wc"), t("u1"), t("u2"), Op.mult)
        segmax(t("ws"), t("rmask", 0, 64), t("wv"))
        ts(t("Wd"), t("Wc"), 0x1FFE0, AND)
        cp(t("woff"), t("ws", 15, 64, 16))
        ts(t(sb, 16, 80), t("Wd"), t("kA"), Op.add)
        send(sb, "LB%d" % r, MSGB, "rb%d" % r)
        if r + 1 < RO:
            for k in range(1, NT):
                mm(t("pY", 64 * k, 64 * k + 64), perm_b(16 - k), t("Yb"))
            act(t("Yr", 64, 512), t("pY", 64, 512), Act.Copy)
        cp(ind(t("tab", 0, 4096), t("woff")), t("Yb"))
        if r + 1 < RO:
            for k in range(1, NT):
                cp(ind(t("tab", 4096 * k, 4096 * k + 4096), t("woff")), t("Yr", 64 * k, 64 * k + 64))
            merge(r)
            names_mul(0)
        else:
            merge(r)
            dma("Y", "d_out", outside(T.yx[:, :]), t("tab", 0, 4096))

    def receive(r):
        lb = "LB%d" % r
        if r + 1 < RO:
            for lo, q, n in ((0, 0, 16), (96, 16, 32), (80, 48, 16)):
                act(t("zb", q, q + n), t(lb, lo, lo + n), Act.Copy)
            mm(t("pV", 64, 128), perm_b(8), t("zb"))
            act(t("z8"), t("pV", 64, 128), Act.Copy)
            act(t("zh"), t("zb"), Act.Copy, scale=0.5, bias=-0.25)
            names_v(0, t(lb, 16, 80), range(4))
            begin(r + 1)
            cp(t("Ai"), t("pU", 64, 65))
            names_v(0, t(lb, 16, 80), range(4, 8))
            ts(t("Aj"), t("Ai"), 31, AND)
            names_mul(1)
            ts(t("ncol"), t("Aj"), -1.0, Op.mult, t("nT"), Op.add)
            names_v(1, t(lb, 16, 80))
            ts(t("thr"), t("tmask"), t("ncol"), Op.mult)
        else:
            for b in range(4):
                s = 16 * ORD[b]
                ts(t("ylf", s, s + 16), t("L16", 16 * b, 16 * b + 16), 2048.0, Op.add)
            dma("Y", "d_out", outside(T.yl[:, :]), t("ylf"))
            for lo, b in ((0, 0), (96, 1), (112, 2), (80, 3)):
                s = 16 * ORD[b]
                act(t("yzf", s, s + 16), t(lb, lo, lo + 16), Act.Copy)
            dma("S", "d_out", outside(T.yz[:, :]), t("yzf"))
            ts(t("Wc"), t(lb, 16, 80), 8388608.0 - 1024.0, Op.add)
            ts(t("Wd"), t("Wc"), 5, SH, 4095, AND)
            for b in range(4):
                s = 16 * ORD[b]
                cp(t("yaf", s, s + 16), t("Wd", 16 * b, 16 * b + 16))
            dma("Y", "d_out", outside(T.ya[:, :]), t("yaf", p0=0, p1=128, ps=16))

    begin(0)
    late_constants()
    for j in range(NV[0]):
        q = NH[0] + j
        ts(t("vd", 128 * j, 128 * j + 64), ind(t("tab", 0, 4 * 4096), off_r(0, 8 * q, 8 * q + 4)), t("zb", q, q + 1), Op.subtract)
    for r in range(RO):
        gathers(r)
        tail(r)
        receive(r)
    for s in sorted(total):
        g.wait_ge(T.sem[s], total[s])
